import numpy as np, ml_dtypes
CORES = [6,15,38,47]
N = 4
BF = ml_dtypes.bfloat16
W, H0, L, RO, Q = 4096, 1024, 256, 3, 3
def base(rng):
    price = rng.integers(0, 101, (N, 8, 1, W)) + rng.integers(0, 28, (N, 8, 16, W))
    packs = rng.integers(0, W, (N, 8, 16, H0)); prev = rng.integers(0, H0, (N, 8, H0)); lots = rng.integers(0, W, (N, 8, 16, L))
    lots[:, :, 0, ::4] = lots[:1, :, 0, ::4]
    o = np.stack([rng.permutation(np.array([5, 20, 35, 50, 60, 70, 80, 90])) for q in range(N)])
    slack = o[:, :, None, None] + rng.integers(0, 9, (N, 8, 16, RO))
    return price, packs, prev, lots, rng.integers(1, 8, (N, 8, 16)), rng.integers(0, 16, (N, 8, 16)), slack
def pack(price, packs, prev, lots, inc, wt, slack):
    c = lambda a, n: np.ascontiguousarray(np.reshape(a, (N, 128, n))).astype(np.int32)
    return {"price": np.ascontiguousarray(price.reshape(N, 128, W)).astype(np.float32).astype(BF), "packs": c(packs, H0), "prev": np.ascontiguousarray(prev).astype(np.int32),
            "lots": c(lots, L), "inc": c(inc, 1), "wt": c(wt, 1), "slack": c(slack, RO)}
def edge(rng, hi, *s):
    return np.where(rng.random(s) < 0.2, rng.integers(0, hi + 1, s), hi * rng.integers(0, 2, s))
def setup_inputs(rng):
    return pack(*base(rng))
def setup_inputs_spread(rng):
    price, packs, prev, lots, inc, wt, slack = base(rng)
    price = np.minimum((np.exp2(7.65 * rng.random((N, 8, 1, W))) * rng.random((N, 8, 16, W))).astype(np.int64), 200)
    packs = np.minimum((W * rng.random((N, 8, 16, H0)) ** 3).astype(np.int64), W - 1)
    lots = W - 1 - np.minimum((W * rng.random((N, 8, 16, L)) ** 2).astype(np.int64), W - 1)
    prev = np.minimum((H0 * rng.random((N, 8, H0)) ** 2).astype(np.int64), H0 - 1)
    slack = np.minimum(np.exp2(8 * rng.random((N, 8, 1, 1)) * rng.random((N, 8, 16, RO))).astype(np.int64) - 1, 255)
    return pack(price, packs, prev, lots, inc, wt, slack)
def setup_inputs_ends(rng):
    hi = np.where(np.arange(8) == 6, 127, 200)[None, :, None, None]
    k = rng.integers(0, 3, (N, 8, 1, W)); price = hi * np.where(k == 2, rng.integers(0, 2, (N, 8, 16, W)), k)
    price[..., 0] = 0; price[..., W - 1] = hi[..., 0]
    price[:, 2:4, :, 0] = 200; price[:, 2:4, :, W - 1] = 0; price[:, 5, 9:, W - 1] = 0
    packs = edge(rng, W - 1, N, 8, 16, H0); prev = edge(rng, H0 - 1, N, 8, H0); lots = edge(rng, W - 1, N, 8, 16, L)
    inc = 1 + 6 * rng.integers(0, 2, (N, 8, 16)); inc[:, 7] = 7; inc[:, 6, 0] = 1
    o = np.argsort(rng.random((N, 8, 16)), axis=2)
    slack = np.repeat((255 * (o >= np.array([16, 9, 16, 9, 12, 16, 8, 8])[None, :, None]))[..., None], RO, axis=3)
    wt = 15 * rng.integers(0, 2, (N, 8, 16)); wt[:, 7] = 0
    full = np.array([15] * 8 + [9] + [0] * 7); wt[:, 6] = full[o[:, 6]]; wt[:, 0] = full[o[:, 0]]
    c = np.array([0, 3, L - 1]); lots[:, 6, 0, c] = W - 1; lots[:, 6, 15, c] = W - 1
    v = np.arange(W)
    back = lambda t, to: int(np.argmax(((v + (v >> 5) + 77 * (t + 1)) & (W - 1)) == to))
    lots[:, 7, 0, c] = W - 1; lots[:, 7, 1, c] = back(0, W - 1); lots[:, 7, 2, c] = back(0, back(1, W - 1))
    return pack(price, packs, prev, lots, inc, wt, slack)
def setup_inputs_corners(rng):
    price, packs, prev, lots, inc, wt, slack = base(rng); a = np.arange(H0)
    kinds = [a, np.maximum(a - 1, 0), 0 * a, 0 * a + H0 - 1, (a + 1) % H0, a ^ 1, H0 - L + a % L]
    for q in range(N):
        for g, k in enumerate(rng.permutation(8)):
            if k < 7: prev[q, g] = kinds[int(k)]
            wt[q, g] = (0, 15, 1, 7)[int(rng.integers(0, 4))] if k < 4 else wt[q, g]
            inc[q, g] = 1 if k % 3 == 0 else 7 if k % 3 == 1 else inc[q, g]
    s = [int(g) for g in rng.permutation(8)]
    for g in s[:4]: slack[:, g] = 255
    lots[:, s[0], :RO] = W - 1; wt[:, s[0]] = 0; price[:, s[0], :, W - 1] = 127; inc[:, s[0]] = 7
    lots[:, s[1], 0] = 0; price[:, s[1], :, 0] = 127 * rng.integers(0, 2, (N, 16))
    m = rng.permutation(W); lots[:, s[2], 0] = m[(np.arange(N * L) % (W - 1) + 1).reshape(N, L)]; lots[int(rng.integers(0, N)), s[2], 0, L - 1] = m[0]
    for q in range(N): lots[q, s[3], 0] = rng.permutation(W)[:L]
    packs[:, s[4], :, H0 - L:] = lots[:, s[4]]
    slack[:, s[4]] = 0; slack[:, s[5]] = 0; h = W // 2
    price[:, s[5], :, :h] = rng.integers(0, 3, (N, 16, h)); price[:, s[5], :, h:] = 127; lots[:, s[5]] = rng.integers(h, W, (N, 16, L)); packs[:, s[5]] = rng.integers(0, h, (N, 16, H0))
    nxt = lambda z, u, t: (((z * (2 * u + 1)) >> 5) + z + 77 * (t + 1)) & (W - 1)
    g = s[6]; b = int(rng.integers(0, N)); k = L // 2
    wt[:, g] = 0; inc[:, g] = 7; inc[b, g] = 1 + rng.permutation(16) % 5
    slack[:, g] = 255; slack[:, g, :, RO - 1] = 254 - rng.integers(0, 55, (N, 16)) * (np.arange(N) % 2)[:, None]
    e = rng.integers(0, W, L); own = nxt(e, 0, 0); own[k:] = nxt(own[k:], 0, 1)
    lots[:, g, 0] = own; lots[:, g, 1, :k] = e[:k]; lots[:, g, 2, k:] = e[k:]
    dear = np.zeros(W, bool); dear[own] = True; low = rng.random(W) < 0.5
    v = 200 - (rng.random((N, 16, W)) * np.where(low, 32, 8)).astype(np.int64)
    v[b] = np.where(low, rng.integers(0, 4, (16, W)), v[b])
    price[:, g] = np.where(dear, v, rng.integers(0, 3, W))
    g = s[7]; wt[:, g] = 15; inc[:, g] = 7; slack[:, g] = 255; price[:, g] = 200
    e = rng.integers(0, W, L); lots[:, g, 1] = e; lots[:, g, 0] = nxt(e, (16 * 15 * 200) & 1023, 0)
    return pack(price, packs, prev, lots, inc, wt, slack)
def setup_inputs_ties(rng):
    price, packs, prev, lots, inc, wt, slack = base(rng)
    s0 = rng.integers(0, 21, (N, 8, 16)); b = rng.integers(0, 106, (N, 8, 16)); slack = np.repeat(s0[..., None], RO, axis=3)
    n = rng.choice(np.array([0, 7, 8, 9, 10, 16]), (N, 8, 1, W)); low = rng.random((N, 8, 1, W)) < 0.5
    o = np.argsort(rng.random((N, 8, W, 16)), axis=3).transpose(0, 1, 3, 2)
    price = b[..., None] + np.where(low, 0, s0[..., None] + (o < n))
    return pack(price, packs, prev, lots, inc, wt, slack)
def check_inputs(d):
    bad = []
    for k, lo, hi in (("price", 0, 200), ("packs", 0, W - 1), ("prev", 0, H0 - 1), ("lots", 0, W - 1), ("inc", 1, 7), ("wt", 0, 15), ("slack", 0, 255)):
        v = np.asarray(d[k]).astype(np.float64)
        if not (np.min(v) >= lo and np.max(v) <= hi): bad.append("range of " + k)
        elif np.any(v != np.floor(v)): bad.append("whole numbers in " + k)
    return bad
def pick(p, t):
    return np.take_along_axis(p, t.reshape(N, 8, 1, 16 * L), 3).reshape(N, 8, 16, 16, L)
def reference(price, packs, prev, lots, inc, wt, slack):
    p = price.astype(np.float32).astype(np.int64).reshape(N, 8, 16, W)
    h = np.zeros((N, 8, 16, H0 + RO * L), np.int64); h[..., :H0] = packs.reshape(N, 8, 16, H0)
    v = np.zeros((N, 8, H0 + RO * L), np.int64); v[..., :H0] = prev
    t = lots.astype(np.int64).reshape(N, 8, 16, L)
    up = inc.astype(np.int64).reshape(N, 8, 16, 1); wr = wt.astype(np.int64).reshape(N, 8, 16, 1); sl = slack.astype(np.int64).reshape(N, 8, 16, RO)
    a = np.zeros((N, 8, L), np.int64) + (H0 - L + np.arange(L))
    for rnd in range(RO):
        x = pick(p, t); bind = np.zeros((N, 8, L), np.int64) - 1
        for e in range(Q):
            anc = np.take_along_axis(h, a[:, :, None, :], 3); y = pick(p, anc)
            rows = np.add.reduce((x - y > sl[:, :, :, rnd][:, :, :, None, None]).astype(np.int64), axis=2)
            rev = rows >= 9
            t = np.where(rev, anc, t); x = np.where(rev[:, :, None], y, x)
            bind = np.where(np.any(rev, axis=2), a, bind); last = a
            a = np.take_along_axis(v, a, 2)
        lo = H0 + L * rnd
        h[..., lo:lo + L] = t; v[..., lo:lo + L] = np.where(bind >= 0, bind, last)
        flag = np.zeros((N, 8, W), np.int64); np.put_along_axis(flag, t[:, :, rnd], 1, 2)
        offer = p * flag[:, :, None]; s = np.add.reduce(offer, axis=0)[None] - offer
        if rnd + 1 < RO:
            u = np.add.reduce(wr * np.max(x, axis=3), axis=2) & 1023
            t = (((t * (2 * u + 1)[:, :, None]) >> 5) + t + 77 * (rnd + 1)) & (W - 1)
            a = np.zeros((N, 8, L), np.int64) + (lo + np.arange(L))
        p = np.minimum(p + ((up * s) >> 6), 255)
    return {"yp": p.reshape(N, 128, W).astype(np.float32).astype(BF), "yh": np.ascontiguousarray(h[..., H0:]).reshape(N, 128, RO * L).astype(np.float32), "yv": np.ascontiguousarray(v[..., H0:]).astype(np.float32)}

@@ -1,0 +1,700 @@
+import numpy as np
+from concourse.bass import DstId, RemoteDMATransfer
+from concourse.mybir import dt, AluOpType, AxisListType, ActivationFunctionType
+
+A = AluOpType
+AF = ActivationFunctionType
+LW = 272
+CH = [(0, 16), (16, 128), (128, 224), (224, 272)]
+NH = len(CH)
+RT = ["vvvvvvssvvvs", "vvvvvvssvvvs", "vvvvvvssvvvs"]
+YR = ["ssssssssssvs", "sssssssssvss", "sssssssvvsss"]
+MR = ["sss", "svs"]
+TG = [[1], [2, 3]]
+NE = 2176
+BIG = 32768.0
+SDUP = (0, 1, 2, 3, 4, 5)
+
+SCRATCH = {
+    "p0": ("sbuf", [128, 4096], "bfloat16"),
+    "F1": ("sbuf", [128, 4352], "float32"),
+    "F2": ("sbuf", [128, 4352], "float32"),
+    "F3": ("sbuf", [128, 4352], "float32"),
+    "pkI": ("sbuf", [128, 768], "int32"),
+    "pkJ": ("sbuf", [128, LW], "int32"),
+    "PK": ("sbuf", [128, 1792], "float32"),
+    "VT": ("sbuf", [128, 1024], "int32"),
+    "small": ("sbuf", [128, 8], "int32"),
+    "slI": ("sbuf", [128, 4], "int32"),
+    "sm": ("sbuf", [128, 32], "float32"),
+    "pI": ("sbuf", [128, 4], "int32"),
+    "row8": ("sbuf", [128, 8], "float32"),
+    "B8": ("sbuf", [128, 8], "float32"),
+    "one16": ("sbuf", [128, 16], "float32"),
+    "SELK": ("sbuf", [128, 2048], "bfloat16"),
+    "SELH": ("sbuf", [128, 2048], "float16"),
+    "ones": ("sbuf", [128, 128], "bfloat16"),
+    "cB": ("sbuf", [128, 384], "bfloat16"),
+    "IDN": ("sbuf", [128, 128], "float32"),
+    "onesF": ("sbuf", [128, 128], "float32"),
+    "IDB": ("sbuf", [128, 256], "bfloat16"),
+    "WT": ("sbuf", [128, 128], "bfloat16"),
+    "TT0": ("sbuf", [128, LW], "uint16"),
+    "TT1": ("sbuf", [128, LW], "uint16"),
+    "A16": ("sbuf", [128, 3 * LW], "uint16"),
+    "AE": ("sbuf", [128, 3 * LW], "float32"),
+    "Wt": ("sbuf", [128, LW], "int32"),
+    "WF": ("sbuf", [128, LW], "float32"),
+    "TI": ("sbuf", [128, LW], "int32"),
+    "TJ": ("sbuf", [128, LW], "int32"),
+    "Y": ("sbuf", [128, 48 * LW], "bfloat16"),
+    "C": ("sbuf", [128, 16 * LW], "bfloat16"),
+    "XS": ("sbuf", [128, 16 * LW], "bfloat16"),
+    "XM": ("sbuf", [128, 4096], "bfloat16"),
+    "SM": ("sbuf", [128, 4096], "bfloat16"),
+    "MK": ("sbuf", [128, 4096], "bfloat16"),
+    "SG": ("sbuf", [128, 768], "bfloat16"),
+    "uI": ("sbuf", [128, 256], "int32"),
+    "uJ": ("sbuf", [128, 256], "int32"),
+    "qF": ("sbuf", [128, 256], "float32"),
+    "qI": ("sbuf", [128, 256], "int32"),
+    "KY": ("sbuf", [128, 3, 32], "float32"),
+    "KB": ("sbuf", [128, 32], "float32"),
+    "KM": ("sbuf", [128, 3, 32], "float32"),
+    "k1": ("sbuf", [128, 32], "float32"),
+    "k2": ("sbuf", [128, 32], "float32"),
+    "kI": ("sbuf", [128, 32], "int32"),
+    "kJ": ("sbuf", [128, 32], "int32"),
+    "kF": ("sbuf", [128, 32], "float32"),
+    "LU": ("sbuf", [128, 64], "uint16"),
+    "i16": ("sbuf", [128, 16], "float32"),
+    "L1c": ("sbuf", [128, 16], "float32"),
+    "VH": ("sbuf", [128, 256], "float16"),
+    "PV": ("sbuf", [128, 48], "float32"),
+    "yvb": ("sbuf", [128, 384], "float32"),
+    "CF": ("sbuf", [128, 16], "float32"),
+    "IDW": ("sbuf", [128, 4096], "float32"),
+    "RH": ("sbuf", [128, 256], "float16"),
+    "RB": ("sbuf", [128, 256], "float32"),
+    "IX": ("sbuf", [128, 256], "float32"),
+    "QM": ("sbuf", [128, 256], "bfloat16"),
+    "EQ": ("sbuf", [128, NE], "bfloat16"),
+    "EM": ("sbuf", [128, NE], "bfloat16"),
+    "SC": ("sbuf", [128, NE], "bfloat16"),
+    "E16": ("sbuf", [128, 2], "uint16"),
+    "DJ": ("sbuf", [128, 16], "float32"),
+    "DJt": ("sbuf", [128, 16], "float32"),
+    "dE": ("sbuf", [128, 16], "float32"),
+    "dF": ("sbuf", [128, 16], "float32"),
+    "dG": ("sbuf", [128, 16], "float32"),
+    "SV": ("sbuf", [128, 768], "bfloat16"),
+    "SL": ("sbuf", [128, 48], "uint16"),
+    "LV": ("sbuf", [128, 3 * 768], "bfloat16"),
+    "LL": ("sbuf", [128, 3 * 64], "uint16"),
+    "sv": ("sbuf", [128, 768], "float32"),
+    "g1": ("sbuf", [128, 512], "float32"),
+    "t1": ("sbuf", [128, 256], "float32"),
+    "i1": ("sbuf", [128, 768], "int32"),
+    "Z0": ("psum", [128, 512], "float32"),
+    "Z1": ("psum", [128, 512], "float32"),
+    "Z2": ("psum", [128, 512], "float32"),
+    "Z3": ("psum", [128, 512], "float32"),
+    "ZT": ("psum", [128, 512], "float32"),
+    "ZX": ("psum", [128, 512], "float32"),
+    "ZB": ("psum", [128, 3, 16], "float32"),
+    "ZM": ("psum", [128, 512], "float32"),
+}
+NDMA = 90
+SEMAPHORES = ["cv", "cs", "cp", "cg", "lsem", "arr0", "arr1", "arr2"] + ["d%d" % i for i in range(NDMA)]
+
+MODELS = [
+    (0.055, 1.04e-3, 1.62e-3, 3.2e-3, 0.60e-3, 0.08, 1.0, 4.5),
+    (0.055, 0.90e-3, 0.95e-3, 1.6e-3, 0.50e-3, 0.05, 0.8, 3.5),
+    (0.060, 1.20e-3, 2.40e-3, 5.5e-3, 0.70e-3, 0.12, 1.3, 7.0),
+    (0.060, 1.10e-3, 1.30e-3, 5.0e-3, 0.60e-3, 0.20, 1.5, 6.0),
+]
+TRIES = 1200
+
+
+def cv(n, per=1.0):
+    return (1.0, max(64, n * per), 0, 0, 0, 0)
+
+
+def cgat(n):
+    return (1.0, 0, n, 0, 0, 0)
+
+
+def csca(n):
+    return (1.0, 0, 0, n, 0, 0)
+
+
+def cmm(n, k=1):
+    return (0.2 * k, 0, 0, 0, k * max(64, n), 0)
+
+
+def cfix(x):
+    return (0, 0, 0, 0, 0, x)
+
+
+def price_ops(ops, md):
+    cost, lat = [], []
+    for o in ops:
+        c = o["cost"]
+        cost.append(c[0] * md[0] + c[1] * md[1] + c[2] * md[2] + c[3] * md[3] + c[4] * md[4] + c[5])
+        lat.append(o["lat"] * (md[6] if o["kind"] == "d" else 1.0) if o["kind"] != "n" else md[7])
+    return cost, lat
+
+
+def run_order(ops, order, cost, lat, wake):
+    free, fin = {}, [0.0] * len(ops)
+    end = 0.0
+    for i in order:
+        o = ops[i]
+        e = o["e"]
+        s = free.get(e, 0.0) if e != "n" else 0.0
+        for p in o["full"]:
+            if fin[p] + wake > s:
+                s = fin[p] + wake
+        f = s + cost[i]
+        free[e] = f
+        fin[i] = f + lat[i]
+        if fin[i] > end:
+            end = fin[i]
+    return end
+
+
+def schedule(ops, succ, prio, cost, lat, wake, window):
+    m = len(ops)
+    left = [len(o["full"]) + len(o["order"]) for o in ops]
+    ready = [0.0] * m
+    free, pend = {}, {}
+    for i, o in enumerate(ops):
+        free[o["e"]] = 0.0
+        pend.setdefault(o["e"], [])
+        if not left[i]:
+            pend[o["e"]].append(i)
+    names = sorted(pend)
+    start = [0.0] * m
+    for _ in range(m):
+        t0, e = 1e30, None
+        for x in names:
+            if pend[x]:
+                t = max(free[x], min(ready[i] for i in pend[x]))
+                if t < t0:
+                    t0, e = t, x
+        i = max((i for i in pend[e] if ready[i] <= t0 + window), key=lambda i: (prio[i], -i))
+        s = max(t0, ready[i])
+        start[i] = s
+        pend[e].remove(i)
+        free[e] = s + cost[i] if e != "n" else 0.0
+        for j, f in succ[i]:
+            ready[j] = max(ready[j], s + cost[i] + (lat[i] + wake if f else 0.0))
+            left[j] -= 1
+            if not left[j]:
+                pend[ops[j]["e"]].append(j)
+    return sorted(range(m), key=lambda i: (start[i], i))
+
+
+PLAN = {}
+
+
+def plan(ops):
+    if "order" in PLAN:
+        return PLAN["order"]
+    m = len(ops)
+    succ = [[] for _ in ops]
+    for i, o in enumerate(ops):
+        for p in o["full"]:
+            succ[p].append((i, True))
+        for p in o["order"]:
+            succ[p].append((i, False))
+    priced = [price_ops(ops, md) for md in MODELS]
+    cost, lat = priced[0]
+    base = [0.0] * m
+    for i in range(m - 1, -1, -1):
+        b = 0.0
+        for j, f in succ[i]:
+            b = max(b, base[j] + (lat[i] + MODELS[0][5] if f else 0.0))
+        base[i] = b + cost[i] + ops[i]["up"]
+    rng = np.random.default_rng(1)
+    ref, best, bestn = None, None, np.zeros(m)
+    for k in range(TRIES):
+        if k < 4:
+            noise, window = np.zeros(m), (0.05, 0.15, 0.3, 0.02)[k]
+        else:
+            noise = bestn + rng.normal(0.0, (12.0, 4.0)[k % 2], m) * (rng.random(m) < (0.1, 0.03, 0.01)[k % 3])
+            window = best[2] if k % 5 else float(rng.choice([0.02, 0.05, 0.1, 0.2]))
+        order = schedule(ops, succ, [base[i] + float(noise[i]) for i in range(m)], cost, lat, MODELS[0][5], window)
+        ts = [run_order(ops, order, c, l, md[5]) for (c, l), md in zip(priced, MODELS)]
+        if ref is None:
+            ref = ts
+        sc = sum(a / b for a, b in zip(ts, ref))
+        if best is None or sc < best[0]:
+            best, bestn = (sc, order, window, ts), noise
+    PLAN["order"] = best[1]
+    PLAN["ts"] = (ref, best[3])
+    return best[1]
+
+
+def rank_program(g, core, T, topo):
+    rank = T.rank_of(core)
+    if rank is None:
+        return
+    n = len(T.cores)
+    Q = {"v": g.vector, "s": g.scalar, "p": g.tensor, "g": g, "y": g.sync}
+    CSEM = {"v": "cv", "s": "cs", "p": "cp", "g": "cg"}
+    ops = []
+    lastw, readers = {}, {}
+
+    def add(e, kind, body, r, w, cost, lat=0.0, up=0.0):
+        i = len(ops)
+        full, order = set(), set()
+        comp = kind == "c"
+        for k in r:
+            if k in lastw:
+                full.add(lastw[k])
+        for k in w:
+            if k in lastw:
+                full.add(lastw[k])
+            for x in readers.get(k, []):
+                if comp and ops[x]["e"] == e and ops[x]["kind"] == "c":
+                    order.add(x)
+                else:
+                    full.add(x)
+        full.discard(i)
+        ops.append({"e": e, "kind": kind, "body": body, "full": sorted(full), "order": sorted(order - full),
+                    "cost": cost, "lat": lat, "up": up})
+        for k in r:
+            readers.setdefault(k, []).append(i)
+        for k in w:
+            lastw[k] = i
+            readers[k] = []
+
+    def V(f, r=(), w=(), c=cv(1)):
+        add("v", "c", [f], r, w, c)
+
+    def S(f, r=(), w=(), c=cv(1)):
+        add("s", "c", [f], r, w, c)
+
+    def PE(fs, r=(), w=(), c=None):
+        fs = fs if isinstance(fs, list) else [fs]
+        add("p", "c", fs, r, w, c if c else cmm(16, len(fs)))
+
+    def G(f, r=(), w=(), c=cfix(0.2)):
+        add("g", "c", [f], r, w, c)
+
+    def dma(e, pairs, r=(), w=(), lat=2.3, up=0.0):
+        add(e, "d", pairs, r, w, cfix(0.06 * len(pairs)), lat, up)
+
+    RF, GF, RQ, INC, WTF, SLF, SB, HF, C14, C15 = 0, 1, 2, 3, 4, 8, 12, 16, 17, 18
+    sm = T.sm
+    col = lambda c: sm[:, c:c + 1]
+    HA = range(NH)
+    HS = range(1, NH)
+    ALL = ["c"] + list(HS)
+    part = lambda h: ["c"] if h == 0 else [h]
+    TT = lambda t: T["TT%d" % (t % 2)]
+    tk = lambda t, hs: ["TT%d_%s" % (t % 2, h) for h in hs]
+    TIB = lambda t: T.TI if t % 2 == 0 else T.TJ
+    ik = lambda t, hs: [("TI_%s" if t % 2 == 0 else "TJ_%s") % h for h in hs]
+    ek = lambda e, hs: ["AE%d_%s" % (e, h) for h in hs]
+    win = lambda t: T.p0[:, 0:4096] if t == 0 else T["F%d" % t][:, 0:4096]
+    wkey = lambda t: ["win%d" % t]
+
+    def alist(t, e, a, b):
+        return TT(t - 1)[:, a:b] if e == 1 and t > 0 else T.A16[:, LW * (e - 1) + a:LW * (e - 1) + b]
+
+    def ak(t, e, hs):
+        return tk(t - 1, hs) if e == 1 and t > 0 else ["A16_%d_%s" % (e, h) for h in hs]
+
+    dma("y", [(T.pkJ[:, 16:LW], T.packs[:, 768:1024]), (T.pkJ[:, 0:16], T.packs[0:128:16, 768:1024])], w=["pkJ"], lat=3, up=2000)
+    dma("y", [(T.slI[:, 0:3], T.slack[:])], w=["slI"], lat=3, up=1800)
+    dma("y", [(T.p0[:], T.price[:])], w=["win0"], lat=6, up=1600)
+    dma("y", [(T.TI[:, 16:LW], T.lots[:]), (T.TI[:, 0:16], T.lots[0:128:16, :])], w=ik(0, ALL), lat=4, up=1500)
+    dma("s", [(T.VT[r:128:16, :], T.prev[:]) for r in range(8)], w=["VTa"], lat=7)
+    dma("y", [(T.VT[r:128:16, :], T.prev[:]) for r in range(8, 16)], w=["VTb"], lat=7)
+    dma("y", [(T.pkI[:], T.packs[:, 0:768])], w=["pkI"], lat=9)
+    dma("y", [(T.small[:, 0:1], T.inc[:]), (T.small[:, 4:5], T.wt[:])], w=["smallI"], lat=9)
+    VTR = ["VTa", "VTb"]
+
+    G(lambda q: q.iota(T.pI[:, 0:1], [[1, 1]], 0, 1), w=["pI"])
+    G(lambda q: q.iota(T.row8[:], [[1, 8]], 0, 0, allow_small_or_imprecise_dtypes=True), w=["row8"])
+    G(lambda q: q.iota(T.i16[:], [[16, 16]], 0, 0, allow_small_or_imprecise_dtypes=True), w=["i16"])
+
+    V(lambda q: q.memset(T.SELK[:], 0.0), w=["SELK"], c=cv(1024))
+    V(lambda q: q.memset(T.one16[:], 1.0), w=["one16"])
+    V(lambda q: q.memset(T.ones[:], 1.0), w=["ones"])
+    for i, x in enumerate((-8.5, -1.0, 15.0)):
+        V(lambda q, i=i, x=x: q.memset(T.cB[:, 128 * i:128 * i + 128], x * BIG), w=["cB%d" % i])
+    V(lambda q: q.tensor_scalar(T.pI[:, 1:2], T.pI[:, 0:1], 15, None, A.bitwise_and), r=["pI"], w=["pI1"])
+    V(lambda q: q.tensor_scalar(T.pI[:, 2:3], T.pI[:, 0:1], 4, None, A.logical_shift_right), r=["pI"], w=["pI2"])
+    V(lambda q: q.tensor_copy(col(RF), T.pI[:, 1:2]), r=["pI1"], w=["RF"])
+    V(lambda q: q.tensor_copy(col(GF), T.pI[:, 2:3]), r=["pI2"], w=["GF"])
+    V(lambda q: q.tensor_scalar(T.B8[:], T.row8[:], col(GF), None, A.is_equal), r=["row8", "GF"], w=["B8"])
+    V(lambda q: q.tensor_scalar(T.L1c[:], T.i16[:], col(RF), None, A.add), r=["i16", "RF"], w=["L1c"])
+    for gg in range(8):
+        V(lambda q, gg=gg: q.tensor_scalar(T.SELK[:, 16 * gg:16 * gg + 129 * 15 + 1:129], T.one16[:],
+                                           T.B8[:, gg:gg + 1], BIG, A.mult, A.mult),
+          r=["one16", "B8", "SELK"], w=["SELK%d" % gg])
+    SELK = ["SELK"] + ["SELK%d" % gg for gg in range(8)]
+    V(lambda q: q.tensor_copy(T.A16[:, 0:LW], T.pkJ[:]), r=["pkJ"], w=ak(0, 1, ALL), c=cv(LW))
+    V(lambda q: q.tensor_copy(sm[:, SLF:SLF + 3], T.slI[:, 0:3]), r=["slI"], w=["SLF"])
+    V(lambda q: q.tensor_copy(T.TT0[:], T.TI[:]), r=ik(0, ALL), w=tk(0, ALL), c=cv(LW))
+    V(lambda q: q.tensor_scalar(T.AE[:, 0:LW], T.pkJ[:], 4096.0, None, A.add), r=["pkJ"], w=ek(1, ALL), c=cv(LW))
+    V(lambda q: q.tensor_copy(T.VH[:], T.VT[:, 768:1024]), r=VTR, w=["VH"], c=cv(256))
+    V(lambda q: q.tensor_scalar(T.SELH[:], T.SELK[:], 1.0 / BIG, None, A.mult), r=SELK, w=["SELH"], c=cv(1024))
+    for e in range(3):
+        V(lambda q, e=e: q.memset(col(SB + e), 0.5 - 4096.0 * (e + 1)), w=["SB%d" % e])
+    V(lambda q: q.memset(col(HF), -0.5), w=["HF"])
+    V(lambda q: q.memset(T.onesF[:], 1.0), w=["onesF"], c=cv(128))
+    G(lambda q: q.affine_select(T.IDB[:, 0:128], T.ones[:], [[-1, 128]], A.is_equal, 0.0, 0, 1), r=["ones"], w=["IDB"], c=cfix(0.45))
+    V(lambda q: q.tensor_scalar(T.IDB[:, 128:256], T.IDB[:, 0:128], -1.0, None, A.mult), r=["IDB"], w=["IDM"])
+    G(lambda q: q.iota(T.IDW[:], [[1, 4096]], -2048, 0, allow_small_or_imprecise_dtypes=True), w=["IDW"], c=cfix(8.5))
+    G(lambda q: q.iota(T.IX[:], [[1, 256]], 0, 0, allow_small_or_imprecise_dtypes=True), w=["IX"], c=cfix(0.7))
+    G(lambda q: q.affine_select(T.IDN[:], T.onesF[:], [[-1, 128]], A.is_equal, 0.0, 0, 1), r=["onesF"], w=["IDN"], c=cfix(0.45))
+    V(lambda q: q.tensor_copy(T.PK[:, 768:1024], T.pkJ[:, 16:LW]), r=["pkJ"], w=["PKb"], c=cv(256))
+    V(lambda q: q.tensor_copy(T.PK[:, 0:768], T.pkI[:]), r=["pkI"], w=["PKa"], c=cv(768))
+    V(lambda q: q.memset(T.F1[:, 4096:4352], 0.0), w=["win1d"], c=cv(256))
+    V(lambda q: q.tensor_scalar(col(RQ), col(RF), 1.0, None, A.add), r=["RF"], w=["RQ"])
+    V(lambda q: q.tensor_scalar(T.QM[:], T.IX[:], col(RQ), 1.0e9, A.is_equal, A.mult), r=["IX", "RQ"], w=["QM"], c=cv(256))
+    seg = [256 * c - 8 * c * (c - 1) for c in range(17)]
+    dma("y", [(T.EM[:, seg[c]:seg[c + 1]], T.QM[:, 0:256 - 16 * c]) for c in range(16)], r=["QM"], w=["EM"])
+    V(lambda q: q.tensor_scalar(col(C14), col(RF), -8.0, 248.0, A.mult, A.add), r=["RF"], w=["c14"])
+    V(lambda q: q.tensor_tensor(col(C15), col(C14), col(RF), A.mult), r=["c14", "RF"], w=["c15"])
+    V(lambda q: q.tensor_scalar(T.E16[:, 0:1], col(C15), 255.0, None, A.add), r=["c15"], w=["E16"])
+    V(lambda q: q.tensor_scalar(T.DJt[:], T.L1c[:], 4096.0, None, A.add), r=["L1c"], w=["DJt"])
+    V(lambda q: q.tensor_scalar(T.dF[:], T.DJt[:], 4350.5, None, A.is_lt), r=["DJt"], w=["dF"])
+    V(lambda q: q.tensor_tensor(T.DJ[:], T.dF[:], T.DJt[:], A.mult), r=["dF", "DJt"], w=["DJ"])
+    V(lambda q: q.tensor_scalar(col(INC), T.small[:, 0:1], 1.0 / 64, None, A.mult), r=["smallI"], w=["INC"])
+    V(lambda q: q.tensor_copy(col(WTF), T.small[:, 4:5]), r=["smallI"], w=["WTF"])
+    V(lambda q: q.memset(T.MK[:], 1.0), w=["MK"], c=cv(2048))
+    V(lambda q: q.memset(T.MK[:, 0:4096:16], 0.0), r=["MK"], w=["MKz"], c=cv(256))
+    for gg in range(8):
+        V(lambda q, gg=gg: q.tensor_scalar(T.WT[:, 16 * gg:16 * gg + 16], T.one16[:], T.B8[:, gg:gg + 1], col(WTF), A.mult, A.mult),
+          r=["one16", "B8", "WTF"], w=["WT%d" % gg])
+    WTR = ["WT%d" % gg for gg in range(8)]
+
+    KY, KB = T.KY, T.KB
+    K2 = [(KY[:, 0, 16:32], "KY01", 4096.0), (KY[:, 1, 0:16], "KY10", 8192.0)]
+    K3 = [(KY[:, 1, 16:32], "KY11", 8192.0), (KY[:, 2, 0:16], "KY20", 12288.0), (KB[:, 0:16], "KB0", 0.0)]
+    K4 = [(KY[:, 2, 16:32], "KY21", 12288.0), (KB[:, 16:32], "KB1", 0.0)]
+
+    def conv(dst, keys):
+        PE([lambda q, k=k: q.matmul(T.ZM[:, 256:272], T.SELH[:, 128 * k:128 * k + 128], T.VH[:, k:256:16], k == 0, k == 15)
+            for k in range(16)], r=["VH", "SELH"], w=["bM"])
+        if dst < 48:
+            V(lambda q: q.tensor_scalar(T.LU[:, dst:dst + 16], T.ZM[:, 256:272], 1.0 / 16, None, A.mult), r=["bM"], w=["LU%d" % dst])
+        V(lambda q: q.tensor_scalar(T.kF[:, 0:16], T.ZM[:, 256:272], 1.0 / 16, None, A.mult), r=["bM"], w=["kF"])
+        for ap, nm, off in keys:
+            S(lambda q, ap=ap, off=off: q.activation(ap, T.kF[:, 0:16], AF.Copy, bias=off), r=["kF"], w=[nm])
+
+    def parents(src):
+        V(lambda q: q.tensor_copy(T.VH[:], T.VT[:, 0:1024].indirect(T.LU[:, src:src + 16])), r=VTR + ["LU%d" % src], w=["VH"], c=cgat(256))
+
+    def newest(t):
+        base = 768.0 + 256 * t
+        S(lambda q: q.activation(KY[:, 0, 0:16], T.L1c[:], AF.Copy, bias=base + 4096.0), r=["L1c"], w=["KY00"])
+
+    def package(t, e):
+        c, b = LW * (e - 1) + 16, 16 * (e - 1)
+        S(lambda q: q.activation(T.AE[:, c:c + 256], T.PK[:, 0:1024 + 256 * t].indirect(T.LU[:, b:b + 16]), AF.Copy, bias=4096.0 * e),
+          r=["PKa", "PKb"] + ["PK%d_%d" % (i, h) for i in range(t) for h in HS] + ["LU%d" % b], w=ek(e, HS), c=cgat(256))
+        V(lambda q: q.tensor_scalar(T.A16[:, c:c + 256], T.AE[:, c:c + 256], -4096.0 * e, None, A.add),
+          r=ek(e, HS), w=ak(t, e, HS), c=cv(256))
+
+    def clist(t, e):
+        if e == 0:
+            dma("y", [(TT(t)[:, 0:16], TT(t)[t:128:16, 16:LW])], r=tk(t, HS), w=tk(t, ["c"]))
+            dma("y", [(TIB(t)[:, 0:16], TIB(t)[t:128:16, 16:LW])], r=ik(t, HS), w=ik(t, ["c"]))
+        else:
+            o = LW * (e - 1)
+            dma("y", [(alist(t, e, 0, 16), alist(t, e, 16, LW)[t:128:16, :])], r=ak(t, e, HS), w=ak(t, e, ["c"]))
+            dma("y", [(T.AE[:, o:o + 16], T.AE[t:128:16, o + 16:o + LW])], r=ek(e, HS), w=ek(e, ["c"]))
+
+    blocks = lambda m: [(x, min(x + 512, 16 * m)) for x in range(0, 16 * m, 512)]
+
+    def gy(t, e, h):
+        a, b = CH[h]
+        o = 16 * (LW * (e - 1) + a)
+        out, lst = T.Y[:, o:o + 16 * (b - a)], win(t).indirect(alist(t, e, a, b))
+        r, w, c = wkey(t) + ak(t, e, part(h)) + ["SLF"], ["Y%d_%d" % (e, h)], cgat(16 * (b - a))
+        if YR[t][NH * (e - 1) + h] == "v":
+            V(lambda q: q.tensor_scalar(out, lst, col(SLF + t), None, A.add), r=r, w=w, c=c)
+        else:
+            S(lambda q: q.activation(out, lst, AF.Identity, bias=col(SLF + t)), r=r, w=w, c=c)
+
+    def gx(t, e, h):
+        a, b = CH[h]
+        o = 16 * LW * (e - 1)
+        c0, c1 = 16 * a, 16 * b
+        m = b - a
+        z = T["Z%d" % h]
+        lst = win(t).indirect(TT(t)[:, a:b])
+        r = wkey(t) + tk(t, part(h))
+        ck = ["C%d_%d" % (h, x) for x, y in blocks(m)]
+        if RT[t][NH * (e - 1) + h] == "v":
+            V(lambda q: q.tensor_tensor(T.C[:, c0:c1], lst, T.Y[:, o + c0:o + c1], A.is_gt), r=r + ["Y%d_%d" % (e, h)], w=ck, c=cgat(16 * m))
+            sh = 0
+        else:
+            S(lambda q: q.activation(T.XS[:, c0:c1], lst, AF.Copy), r=r, w=["XS%d" % h], c=cgat(16 * m))
+            for x, y in blocks(m):
+                PE([lambda q, x=x, y=y: q.matmul(T.ZX[:, 0:y - x], T.IDB[:, 0:128], T.XS[:, c0 + x:c0 + y], True, False),
+                    lambda q, x=x, y=y: q.matmul(T.ZX[:, 0:y - x], T.IDB[:, 128:256], T.Y[:, o + c0 + x:o + c0 + y], False, True)],
+                   r=["XS%d" % h, "IDB", "IDM", "Y%d_%d" % (e, h)], w=["bX"], c=cmm(y - x, 2))
+                S(lambda q, x=x, y=y: q.activation(T.C[:, c0 + x:c0 + y], T.ZX[:, 0:y - x], AF.Sign, bias=col(HF)),
+                  r=["bX", "HF"], w=["C%d_%d" % (h, x)], c=cv(y - x))
+            sh = 1
+        PE([lambda q: q.matmul(z[:, 0:m], T.cB[0:1, 128 * sh:128 * sh + 128], T.ones[0:1, 0:m], True, False)] +
+           [lambda q, k=k: q.matmul(z[:, 0:m], T.SELK[:, 128 * k:128 * k + 128], T.C[:, c0 + k:c1:16], False, k == 15)
+            for k in range(16)], r=ck + ["cB%d" % sh, "ones"] + SELK, w=["bZ%d" % h], c=cmm(m, 17))
+
+    def tops(t, e, h):
+        a, b = CH[h]
+        m = b - a
+        z, ti = T["Z%d" % h], TIB(t)
+        o = LW * (e - 1)
+        V(lambda q: q.tensor_tensor(T.ZT[:, a:b], z[:, 0:m], T.AE[:, o + a:o + b], A.min), r=["bZ%d" % h] + ek(e, part(h)), w=["bT%d" % h], c=cv(m))
+        cur, ck = (ti, ik(t, part(h))) if e == 1 else (T.Wt, ["W%d" % h])
+        if e < 3 or h == 0:
+            V(lambda q: q.tensor_tensor(T.Wt[:, a:b], T.ZT[:, a:b], cur[:, a:b], A.max), r=["bT%d" % h] + ck, w=["W%d" % h], c=cv(m))
+        else:
+            V(lambda q: q.tensor_tensor(T.WF[:, a:b], T.ZT[:, a:b], cur[:, a:b], A.max), r=["bT%d" % h] + ck, w=["WF%d" % h], c=cv(m))
+            V(lambda q: q.tensor_copy(T.Wt[:, a:b], T.WF[:, a:b]), r=["WF%d" % h], w=["W%d" % h], c=cv(m))
+        V(lambda q: q.tensor_scalar(ti[:, a:b], T.Wt[:, a:b], 4095, None, A.bitwise_and), r=["W%d" % h], w=ik(t, part(h)), c=cv(m))
+        V(lambda q: q.tensor_copy(TT(t)[:, a:b], ti[:, a:b]), r=ik(t, part(h)), w=tk(t, part(h)), c=cv(m))
+
+    def fin(t, h):
+        a, b = CH[h]
+        p = 1024 + 256 * t - 16
+        V(lambda q: q.tensor_copy(T.PK[:, p + a:p + b], TIB(t)[:, a:b]), r=ik(t, [h]), w=["PK%d_%d" % (t, h)], c=cv(b - a))
+        if t < 2:
+            S(lambda q: q.activation(T.AE[:, a:b], T.PK[:, p + a:p + b], AF.Copy, bias=4096.0), r=["PK%d_%d" % (t, h)], w=ek(1, [h]), c=cv(b - a))
+        for e in range(3):
+            S(lambda q, e=e: q.activation(T.SG[:, 256 * e + a - 16:256 * e + b - 16], T.WF[:, a:b], AF.Sign, bias=col(SB + e)),
+              r=["WF%d" % h, "SB%d" % e], w=["SG%d_%d" % (e, h)], c=cv(b - a))
+
+    def gm(t, h):
+        a, b = CH[h]
+        x, y = 16 * (a - 16), 16 * (b - 16)
+        lst = win(t).indirect(TT(t)[:, a:b])
+        r, w, c = wkey(t) + tk(t, [h]), ["XM%d" % h], cgat(y - x)
+        if MR[t][h - 1] == "v":
+            V(lambda q: q.tensor_copy(T.XM[:, x:y], lst), r=r, w=w, c=c)
+        else:
+            S(lambda q: q.activation(T.XM[:, x:y], lst, AF.Copy), r=r, w=w, c=c)
+        V(lambda q: q.tensor_tensor_scan(T.SM[:, x:y], T.MK[:, x:y], T.XM[:, x:y], 0.0, A.mult, A.max),
+          r=["MK", "MKz", "XM%d" % h], w=["SM%d" % h], c=cv((y - x) // 2))
+
+    def tnew(t, hs):
+        a, b = CH[hs[0]][0], CH[hs[-1]][1]
+        x, y = a - 16, b - 16
+        m = b - a
+        nm = str(hs[0])
+        uk = ["bT%d" % h for h in hs]
+        PE(lambda q: q.matmul(T.ZM[:, x:y], T.WT[:], T.SM[:, 16 * x + 15:16 * y:16], True, True), r=WTR + ["SM%d" % h for h in hs], w=["bM"], c=cmm(m))
+        V(lambda q: q.tensor_copy(T.uI[:, x:y], T.ZM[:, x:y]), r=["bM"], w=["uI" + nm], c=cv(m))
+        V(lambda q: q.tensor_scalar(T.uJ[:, x:y], T.uI[:, x:y], 1023, None, A.bitwise_and), r=["uI" + nm], w=["uJ" + nm], c=cv(m))
+        V(lambda q: q.tensor_scalar(T.ZT[:, a:b], T.uJ[:, x:y], 2.0, 33.0, A.mult, A.add), r=["uJ" + nm], w=uk, c=cv(m))
+        V(lambda q: q.tensor_tensor(T.qF[:, x:y], T.ZT[:, a:b], TIB(t)[:, a:b], A.mult), r=uk + ik(t, hs), w=["qF" + nm], c=cv(m))
+        V(lambda q: q.tensor_scalar(T.qI[:, x:y], T.qF[:, x:y], 2464.0 * (t + 1), None, A.add), r=["qF" + nm], w=["qI" + nm], c=cv(m))
+        V(lambda q: q.tensor_scalar(TIB(t + 1)[:, a:b], T.qI[:, x:y], 5, 4095, A.logical_shift_right, A.bitwise_and),
+          r=["qI" + nm], w=ik(t + 1, hs), c=cv(m))
+        V(lambda q: q.tensor_copy(TT(t + 1)[:, a:b], TIB(t + 1)[:, a:b]), r=ik(t + 1, hs), w=tk(t + 1, hs), c=cv(m))
+
+    def bind(t):
+        PE([lambda q: q.matmul(T.ZB[:], T.cB[0:1, 256:384], T.ones[0:1, 0:48], True, False)] +
+           [lambda q, k=k: q.matmul(T.ZB[:], T.SELK[:, 128 * k:128 * k + 128], T.SG[:, k:768:16], False, k == 15) for k in range(16)],
+           r=["SG%d_%d" % (e, h) for e in range(3) for h in HS] + SELK + ["cB2", "ones"], w=["bB"])
+        c = 16 if t == 2 else 32
+        ds = range(c // 16)
+        for d in ds:
+            V(lambda q, d=d: q.tensor_tensor(T.KM[:, :, 16 * d:16 * d + 16], T.ZB[:], KY[:, :, 16 * d:16 * d + 16], A.min),
+              r=["bB"] + ["KY%d%d" % (e, d) for e in range(3)], w=["KM%d" % d])
+        V(lambda q: q.tensor_tensor(T.k1[:, 0:c], T.KM[:, 0, 0:c], T.KM[:, 1, 0:c], A.max), r=["KM%d" % d for d in ds], w=["k1"])
+        V(lambda q: q.tensor_tensor(T.k2[:, 0:c], T.k1[:, 0:c], T.KM[:, 2, 0:c], A.max), r=["k1"] + ["KM%d" % d for d in ds], w=["k2"])
+        V(lambda q: q.tensor_tensor(T.kI[:, 0:c], T.k2[:, 0:c], KB[:, 0:c], A.max), r=["k2"] + ["KB%d" % d for d in ds], w=["kI"])
+        V(lambda q: q.tensor_scalar(T.kJ[:, 0:c], T.kI[:, 0:c], 4095, None, A.bitwise_and), r=["kI"], w=["kJ"])
+        if t < 2:
+            V(lambda q: q.tensor_copy(T.LU[:, 16:48], T.kJ[:]), r=["kJ"], w=["LU16", "LU32"])
+            V(lambda q: q.tensor_copy(T.kF[:], T.kJ[:]), r=["kJ"], w=["kF"])
+            S(lambda q: q.activation(T.PV[:, 16 * t:16 * t + 16], T.kF[:, 0:16], AF.Copy), r=["kF"], w=["PV%d" % t])
+            S(lambda q: q.activation(KY[:, 0, 16:32], T.kF[:, 0:16], AF.Copy, bias=4096.0), r=["kF"], w=["KY01"])
+            S(lambda q: q.activation(KY[:, 1, :], T.kF[:], AF.Copy, bias=8192.0), r=["kF"], w=["KY10", "KY11"])
+            S(lambda q: q.activation(KY[:, 2, 0:16], T.kF[:, 16:32], AF.Copy, bias=12288.0), r=["kF"], w=["KY20"])
+            S(lambda q: q.activation(KB[:, 0:16], T.kF[:, 16:32], AF.Copy), r=["kF"], w=["KB0"])
+            newest(t + 1)
+        else:
+            V(lambda q: q.tensor_copy(T.PV[:, 32:48], T.kJ[:, 0:16]), r=["kJ"], w=["PV2"])
+
+    def outv(t):
+        PE(lambda q: q.matmul(T.ZM[0:16, 384:512], T.PV[:, 16 * t:16 * t + 16], T.IDN[:], True, True), r=["PV%d" % t, "IDN"], w=["bM"], c=cmm(128, 4))
+        V(lambda q: q.tensor_copy(T.yvb[0:16, 128 * t:128 * t + 128], T.ZM[0:16, 384:512]), r=["bM"], w=["yvb%d" % t], c=cv(128))
+        for i, e in enumerate(("y", "s") if t == 2 else ("y",)):
+            gs = range(8)[i::2] if t == 2 else range(8)
+            dma(e, [(T.yv[gg:gg + 1, 256 * t:256 * t + 256], T.yvb[0:16, 128 * t + 16 * gg:128 * t + 16 * gg + 16]) for gg in gs],
+                r=["yvb%d" % t], w=["yv%d_%d" % (t, i)])
+
+    def outh(t, hs):
+        a, b = CH[hs[0]][0] - 16, CH[hs[-1]][1] - 16
+        p = 1024 + 256 * t
+        dma("y", [(T.yh[:, 256 * t + a:256 * t + b], T.PK[:, p + a:p + b])], r=["PK%d_%d" % (t, h) for h in hs], w=["yh%d_%d" % (t, a)])
+
+    def dedupe(t):
+        cl, ci, ck, cik = TT(t)[:, 0:16], TIB(t)[:, 0:16], tk(t, ["c"]), ik(t, ["c"])
+        S(lambda q: q.activation(T.SV[:, 256 * t:256 * t + 256], win(t).indirect(cl), AF.Copy), r=wkey(t) + ck, w=["SV%d" % t], c=cgat(256))
+        V(lambda q: q.tensor_copy(T.RH[:], T.IDW[:].indirect(cl)), r=["IDW"] + ck, w=["RH"], c=cgat(256))
+        if SDUP:
+            S(lambda q: q.activation(T.RB[:], T.IDW[:].indirect(cl), AF.Copy), r=["IDW"] + ck, w=["RB"], c=cgat(256))
+        V(lambda q: q.tensor_scalar(T.CF[:], ci, -1.0, 2048.0, A.mult, A.add), r=cik, w=["CF"])
+        for c in range(16):
+            if c in SDUP:
+                S(lambda q, c=c: q.activation(T.EQ[:, seg[c]:seg[c + 1]], T.RB[:, 16 * c:256], AF.Square, bias=T.CF[:, c:c + 1]),
+                  r=["RB", "CF"], w=["EQ%d" % c], c=cv(256 - 16 * c))
+            else:
+                V(lambda q, c=c: q.tensor_scalar(T.EQ[:, seg[c]:seg[c + 1]], T.RH[:, 16 * c:256], T.CF[:, c:c + 1], 0.0, A.add, A.not_equal),
+                  r=["RH", "CF"], w=["EQ%d" % c], c=cv(256 - 16 * c, .5))
+        V(lambda q: q.tensor_tensor_scan(T.SC[:], T.EM[:], T.EQ[:], 1.0e9, A.max, A.min), r=["EM"] + ["EQ%d" % c for c in range(16)], w=["SC"], c=cv(NE, .5))
+        V(lambda q: q.tensor_scalar(T.dE[:], T.SC[:].indirect(T.E16[:, 0:1]), 0.5, None, A.is_lt), r=["SC", "E16"], w=["dE"])
+        V(lambda q: q.tensor_tensor(T.dF[:], T.dE[:], T.DJ[:], A.mult), r=["dE", "DJ"], w=["dF"])
+        V(lambda q: q.tensor_tensor(T.dG[:], T.dF[:], ci, A.max), r=["dF"] + cik, w=["dG"])
+        V(lambda q: q.tensor_copy(T.SL[:, 16 * t:16 * t + 16], T.dG[:]), r=["dG"], w=["SL%d" % t])
+
+    others = [d for d in range(n) if d != rank]
+    common = [e for e in topo.engines(core, T.cores[others[0]]) if all(e in topo.engines(core, T.cores[d]) for d in others)]
+    mask = sum(1 << e for e in common)
+
+    def send(t):
+        for key, buf, land, w, st in (("SV%d" % t, T.SV, T.LV, 256, 768), ("SL%d" % t, T.SL, T.LL, 16, 64)):
+            ids, dsts = [], []
+            for d in others:
+                rid, pid = topo.addr(T.cores[d])[0:2]
+                slot = (rank - d - 1) % n
+                ids.append(DstId(rid=rid, pnc=pid))
+                dsts.append(land[:, st * t + w * slot:st * t + w * slot + w])
+            tr = RemoteDMATransfer(dst_ids=ids, dma_engine_mask=mask, remote_sem=T.sem["arr%d" % t],
+                                   srcs=[buf[:, w * t:w * t + w]], dsts=dsts, alu_op=0)
+            add("g", "r", tr, [key], ["sent" + key], cfix(1.0))
+        add("n", "n", ("arr%d" % t, 2 * len(common) * len(others)), ["sentSV%d" % t, "sentSL%d" % t], ["LV%d" % t], cfix(0.0), 1.0)
+
+    def update(t):
+        F = T["F%d" % (t + 1)]
+        fk = "win%d" % (t + 1)
+        L = lambda a, b: T.LL[:, 64 * t + 16 * a:64 * t + 16 * b]
+        lk = "LV%d" % t
+        cols = lambda i: slice(256 * i, 256 * i + 256)
+        S(lambda q: q.activation(T.sv[:], T.LV[:, 768 * t:768 * t + 768], AF.Copy, scale=col(INC)), r=[lk, "INC"], w=["sv"], c=cv(768))
+        fr = [fk, "win1d", lk] if t == 0 else [fk, lk]
+        for i in range(2):
+            S(lambda q, i=i: q.activation(T.g1[:, cols(i)], F[:].indirect(L(i, i + 1)), AF.Copy), r=fr, w=["g1_%d" % i], c=cgat(256))
+            V(lambda q, i=i: q.tensor_tensor(F[:].indirect(L(i, i + 1)), T.g1[:, cols(i)], T.sv[:, cols(i)], A.add), r=["g1_%d" % i, "sv", lk], w=[fk], c=csca(256))
+        V(lambda q: q.tensor_tensor(T.t1[:], F[:].indirect(L(2, 3)), T.sv[:, 512:768], A.add), r=fr + ["sv"], w=["t1"], c=cgat(256))
+        V(lambda q: q.tensor_scalar(T.i1[:, 512:768], T.t1[:], -0.4921875, 255.0, A.add, A.min), r=["t1"], w=["i1b"], c=cv(256))
+        V(lambda q: q.tensor_copy(F[:].indirect(L(2, 3)), T.i1[:, 512:768]), r=["i1b", lk], w=[fk], c=csca(256))
+        V(lambda q: q.tensor_scalar(T.i1[:, 0:512], F[:].indirect(L(0, 2)), -0.4921875, 255.0, A.add, A.min), r=[fk, lk], w=["i1a"], c=cgat(512))
+        for i in range(2):
+            V(lambda q, i=i: q.tensor_copy(F[:].indirect(L(i, i + 1)), T.i1[:, cols(i)]), r=["i1a", lk], w=[fk], c=csca(256))
+
+    newest(0)
+    conv(16, K2)
+    parents(16)
+    conv(32, K3)
+    package(0, 2)
+    package(0, 3)
+    clist(0, 2)
+    clist(0, 3)
+    for t in range(3):
+        late = tk(t, ["c"]) + ik(t, ["c"]) + [k for e in (1, 2, 3) for k in ak(t, e, ["c"]) + ek(e, ["c"])]
+        if t == 0:
+            dma("g", [(T.F1[:, 0:4096], T.price[:])], r=["win0"] + late, w=["win1"], lat=10)
+        else:
+            dma("y", [(T["F%d" % (t + 1)][:], T["F%d" % t][:])], r=["win%d" % t] + late + (["win1d"] if t == 1 else []), w=["win%d" % (t + 1)], lat=8)
+        for e in (1, 2, 3):
+            for h in HA:
+                gy(t, e, h)
+            for h in HA:
+                gx(t, e, h)
+            for h in HA:
+                tops(t, e, h)
+        dedupe(t)
+        send(t)
+        if t < 2:
+            parents(32)
+            conv(48, K4)
+        update(t)
+        if t == 2:
+            dma("g", [(T.yp[:], T.F3[:, 0:4096])], r=["win3"], w=["yp"], lat=9)
+        for h in HS:
+            fin(t, h)
+        if t < 2:
+            for h in HS:
+                gm(t, h)
+            for hs in TG:
+                tnew(t, hs)
+            clist(t + 1, 1)
+            clist(t + 1, 0)
+            outh(t, list(HS))
+        else:
+            for h in HS:
+                outh(t, [h])
+        bind(t)
+        outv(t)
+        if t < 2:
+            package(t + 1, 2)
+            package(t + 1, 3)
+            clist(t + 1, 2)
+            clist(t + 1, 3)
+
+    order = plan(ops)
+    total, snap, tok = {}, {}, {}
+    seen = {e: {} for e in Q}
+    nd = [0]
+
+    def merge(d, s, v):
+        if d.get(s, 0) < v:
+            d[s] = v
+
+    def sync(e, toks):
+        best = {}
+        for s, v in toks:
+            if seen[e].get(s, 0) < v:
+                merge(best, s, v)
+        for s in sorted(best):
+            if any(o != s and best[o] and snap.get((o, best[o]), {}).get(s, 0) >= best[s] for o in best):
+                best[s] = 0
+        for s in sorted(best):
+            v = best[s]
+            if v:
+                Q[e].wait_ge(T.sem[s], v)
+                merge(seen[e], s, v)
+                for o, w in snap.get((s, v), {}).items():
+                    merge(seen[e], o, w)
+
+    for i in order:
+        o = ops[i]
+        e, kind, body = o["e"], o["kind"], o["body"]
+        if kind == "n":
+            total[body[0]] = body[1]
+            tok[i] = body
+            continue
+        sync(e, [tok[p] for p in o["full"] if p in tok])
+        if kind == "c":
+            s = CSEM[e]
+            for f in body:
+                f(Q[e]).then_inc(T.sem[s], 1)
+                total[s] = total.get(s, 0) + 1
+                snap[(s, total[s])] = dict(seen[e])
+            tok[i] = (s, total[s])
+        elif kind == "d":
+            s = "d%d" % nd[0]
+            nd[0] += 1
+            for out, in_ in body:
+                Q[e].dma_start(out, in_).then_inc(T.sem[s], 16)
+            total[s] = 16 * len(body)
+            tok[i] = (s, total[s])
+            snap[tok[i]] = dict(seen[e])
+        else:
+            g.remote_dma_fused([body], local_sem=T.sem.lsem)
+            total["lsem"] = total.get("lsem", 0) + len(common)
+    for s in sorted(total):
+        if seen["g"].get(s, 0) < total[s]:
+            g.wait_ge(T.sem[s], total[s])

@@ -5,15 +5,15 @@ from concourse.mybir import dt, AluOpType, AxisListType, ActivationFunctionType
 A = AluOpType
 AF = ActivationFunctionType
 LW = 272
-CH = [(0, 16), (16, 128), (128, 224), (224, 272)]
+CH = [(0, 16), (16, 104), (104, 192), (192, 272)]
 NH = len(CH)
-RT = ["vvvvvvssvvvs", "vvvvvvssvvvs", "vvvvvvssvvvs"]
-YR = ["ssssssssssvs", "sssssssssvss", "sssssssvvsss"]
-MR = ["sss", "svs"]
+RT = ["svvvvvssvvvv", "vvvvvvssvvvv", "vvvvvvssvvvv"]
+YR = ["sssssssvssss", "ssssvssvssss", "ssssvssssvsv"]
+MR = ["vss", "sss"]
 TG = [[1], [2, 3]]
 NE = 2176
 BIG = 32768.0
-SDUP = (0, 1, 2, 3, 4, 5)
+SDUP = (0, 1, 2, 3, 4, 5, 6, 7)
 
 SCRATCH = {
     "p0": ("sbuf", [128, 4096], "bfloat16"),
@@ -38,6 +38,8 @@ SCRATCH = {
     "IDN": ("sbuf", [128, 128], "float32"),
     "onesF": ("sbuf", [128, 128], "float32"),
     "IDB": ("sbuf", [128, 256], "bfloat16"),
+    "BD": ("sbuf", [128, 128], "bfloat16"),
+    "BE": ("sbuf", [128, 128], "bfloat16"),
     "WT": ("sbuf", [128, 128], "bfloat16"),
     "TT0": ("sbuf", [128, LW], "uint16"),
     "TT1": ("sbuf", [128, LW], "uint16"),
@@ -74,7 +76,6 @@ SCRATCH = {
     "yvb": ("sbuf", [128, 384], "float32"),
     "CF": ("sbuf", [128, 16], "float32"),
     "IDW": ("sbuf", [128, 4096], "float32"),
-    "RH": ("sbuf", [128, 256], "float16"),
     "RB": ("sbuf", [128, 256], "float32"),
     "IX": ("sbuf", [128, 256], "float32"),
     "QM": ("sbuf", [128, 256], "bfloat16"),
@@ -108,12 +109,14 @@ NDMA = 90
 SEMAPHORES = ["cv", "cs", "cp", "cg", "lsem", "arr0", "arr1", "arr2"] + ["d%d" % i for i in range(NDMA)]
 
 MODELS = [
-    (0.055, 1.04e-3, 1.62e-3, 3.2e-3, 0.60e-3, 0.08, 1.0, 4.5),
-    (0.055, 0.90e-3, 0.95e-3, 1.6e-3, 0.50e-3, 0.05, 0.8, 3.5),
-    (0.060, 1.20e-3, 2.40e-3, 5.5e-3, 0.70e-3, 0.12, 1.3, 7.0),
-    (0.060, 1.10e-3, 1.30e-3, 5.0e-3, 0.60e-3, 0.20, 1.5, 6.0),
+    (0.050, 0.92e-3, 1.35e-3, 2.8e-3, 0.70e-3, 0.08, 1.0, 4.5),
+    (0.045, 0.84e-3, 0.95e-3, 1.6e-3, 0.60e-3, 0.05, 0.8, 3.5),
+    (0.055, 1.20e-3, 2.40e-3, 5.5e-3, 0.95e-3, 0.10, 1.3, 7.0),
+    (0.050, 1.10e-3, 1.40e-3, 5.5e-3, 0.60e-3, 0.18, 0.8, 5.0),
+    (0.060, 1.00e-3, 1.90e-3, 2.0e-3, 0.80e-3, 0.05, 1.0, 4.0),
+    (0.065, 1.10e-3, 1.20e-3, 3.0e-3, 0.90e-3, 0.12, 1.0, 6.0),
 ]
-TRIES = 1200
+TRIES = 1500
 
 
 def cv(n, per=1.0):
@@ -216,13 +219,13 @@ def plan(ops):
         for j, f in succ[i]:
             b = max(b, base[j] + (lat[i] + MODELS[0][5] if f else 0.0))
         base[i] = b + cost[i] + ops[i]["up"]
-    rng = np.random.default_rng(1)
+    rng = np.random.default_rng(2)
     ref, best, bestn = None, None, np.zeros(m)
     for k in range(TRIES):
         if k < 4:
             noise, window = np.zeros(m), (0.05, 0.15, 0.3, 0.02)[k]
         else:
-            noise = bestn + rng.normal(0.0, (12.0, 4.0)[k % 2], m) * (rng.random(m) < (0.1, 0.03, 0.01)[k % 3])
+            noise = bestn + rng.normal(0.0, (40.0, 8.0)[k % 2], m) * (rng.random(m) < (0.1, 0.03, 0.01)[k % 3])
             window = best[2] if k % 5 else float(rng.choice([0.02, 0.05, 0.1, 0.2]))
         order = schedule(ops, succ, [base[i] + float(noise[i]) for i in range(m)], cost, lat, MODELS[0][5], window)
         ts = [run_order(ops, order, c, l, md[5]) for (c, l), md in zip(priced, MODELS)]
@@ -246,11 +249,11 @@ def rank_program(g, core, T, topo):
     ops = []
     lastw, readers = {}, {}
 
-    def add(e, kind, body, r, w, cost, lat=0.0, up=0.0):
+    def add(e, kind, body, r, w, cost, lat=0.0, up=0.0, after=()):
         i = len(ops)
         full, order = set(), set()
         comp = kind == "c"
-        for k in r:
+        for k in list(r) + list(after):
             if k in lastw:
                 full.add(lastw[k])
         for k in w:
@@ -280,11 +283,11 @@ def rank_program(g, core, T, topo):
         fs = fs if isinstance(fs, list) else [fs]
         add("p", "c", fs, r, w, c if c else cmm(16, len(fs)))
 
-    def G(f, r=(), w=(), c=cfix(0.2)):
-        add("g", "c", [f], r, w, c)
+    def G(f, r=(), w=(), c=cfix(0.2), after=()):
+        add("g", "c", [f], r, w, c, after=after)
 
-    def dma(e, pairs, r=(), w=(), lat=2.3, up=0.0):
-        add(e, "d", pairs, r, w, cfix(0.06 * len(pairs)), lat, up)
+    def dma(e, pairs, r=(), w=(), lat=2.3, up=0.0, after=()):
+        add(e, "d", pairs, r, w, cfix(0.06 * len(pairs)), lat, up, after)
 
     RF, GF, RQ, INC, WTF, SLF, SB, HF, C14, C15 = 0, 1, 2, 3, 4, 8, 12, 16, 17, 18
     sm = T.sm
@@ -309,7 +312,7 @@ def rank_program(g, core, T, topo):
 
     dma("y", [(T.pkJ[:, 16:LW], T.packs[:, 768:1024]), (T.pkJ[:, 0:16], T.packs[0:128:16, 768:1024])], w=["pkJ"], lat=3, up=2000)
     dma("y", [(T.slI[:, 0:3], T.slack[:])], w=["slI"], lat=3, up=1800)
-    dma("y", [(T.p0[:], T.price[:])], w=["win0"], lat=6, up=1600)
+    dma("y", [(T.p0[:], T.price[:])], w=["win0"], lat=5, up=1600)
     dma("y", [(T.TI[:, 16:LW], T.lots[:]), (T.TI[:, 0:16], T.lots[0:128:16, :])], w=ik(0, ALL), lat=4, up=1500)
     dma("s", [(T.VT[r:128:16, :], T.prev[:]) for r in range(8)], w=["VTa"], lat=7)
     dma("y", [(T.VT[r:128:16, :], T.prev[:]) for r in range(8, 16)], w=["VTb"], lat=7)
@@ -367,12 +370,9 @@ def rank_program(g, core, T, topo):
     V(lambda q: q.tensor_tensor(T.DJ[:], T.dF[:], T.DJt[:], A.mult), r=["dF", "DJt"], w=["DJ"])
     V(lambda q: q.tensor_scalar(col(INC), T.small[:, 0:1], 1.0 / 64, None, A.mult), r=["smallI"], w=["INC"])
     V(lambda q: q.tensor_copy(col(WTF), T.small[:, 4:5]), r=["smallI"], w=["WTF"])
-    V(lambda q: q.memset(T.MK[:], 1.0), w=["MK"], c=cv(2048))
-    V(lambda q: q.memset(T.MK[:, 0:4096:16], 0.0), r=["MK"], w=["MKz"], c=cv(256))
-    for gg in range(8):
-        V(lambda q, gg=gg: q.tensor_scalar(T.WT[:, 16 * gg:16 * gg + 16], T.one16[:], T.B8[:, gg:gg + 1], col(WTF), A.mult, A.mult),
-          r=["one16", "B8", "WTF"], w=["WT%d" % gg])
-    WTR = ["WT%d" % gg for gg in range(8)]
+    G(lambda q: q.affine_select(T.BD[:], T.ones[:], [[-16, 8], [0, 16]], A.is_ge, 0.0, 0, 1), r=["ones"], w=["BD"], c=cfix(0.45))
+    G(lambda q: q.affine_select(T.BE[:], T.BD[:], [[16, 8], [0, 16]], A.is_ge, 0.0, 15, -1), r=["BD"], w=["BE"], c=cfix(0.45))
+    V(lambda q: q.tensor_scalar(T.WT[:], T.BE[:], col(WTF), None, A.mult), r=["BE", "WTF"], w=["WT"])
 
     KY, KB = T.KY, T.KB
     K2 = [(KY[:, 0, 16:32], "KY01", 4096.0), (KY[:, 1, 0:16], "KY10", 8192.0)]
@@ -482,8 +482,8 @@ def rank_program(g, core, T, topo):
             V(lambda q: q.tensor_copy(T.XM[:, x:y], lst), r=r, w=w, c=c)
         else:
             S(lambda q: q.activation(T.XM[:, x:y], lst, AF.Copy), r=r, w=w, c=c)
-        V(lambda q: q.tensor_tensor_scan(T.SM[:, x:y], T.MK[:, x:y], T.XM[:, x:y], 0.0, A.mult, A.max),
-          r=["MK", "MKz", "XM%d" % h], w=["SM%d" % h], c=cv((y - x) // 2))
+        V(lambda q: q.tensor_tensor_scan(T.SM[:, x:y], T.MK[:, x:y], T.XM[:, x:y], 0.0, A.min, A.max),
+          r=["MK", "XM%d" % h], w=["SM%d" % h], c=cv((y - x) // 2))
 
     def tnew(t, hs):
         a, b = CH[hs[0]][0], CH[hs[-1]][1]
@@ -491,7 +491,7 @@ def rank_program(g, core, T, topo):
         m = b - a
         nm = str(hs[0])
         uk = ["bT%d" % h for h in hs]
-        PE(lambda q: q.matmul(T.ZM[:, x:y], T.WT[:], T.SM[:, 16 * x + 15:16 * y:16], True, True), r=WTR + ["SM%d" % h for h in hs], w=["bM"], c=cmm(m))
+        PE(lambda q: q.matmul(T.ZM[:, x:y], T.WT[:], T.SM[:, 16 * x + 15:16 * y:16], True, True), r=["WT"] + ["SM%d" % h for h in hs], w=["bM"], c=cmm(m))
         V(lambda q: q.tensor_copy(T.uI[:, x:y], T.ZM[:, x:y]), r=["bM"], w=["uI" + nm], c=cv(m))
         V(lambda q: q.tensor_scalar(T.uJ[:, x:y], T.uI[:, x:y], 1023, None, A.bitwise_and), r=["uI" + nm], w=["uJ" + nm], c=cv(m))
         V(lambda q: q.tensor_scalar(T.ZT[:, a:b], T.uJ[:, x:y], 2.0, 33.0, A.mult, A.add), r=["uJ" + nm], w=uk, c=cv(m))
@@ -542,17 +542,15 @@ def rank_program(g, core, T, topo):
     def dedupe(t):
         cl, ci, ck, cik = TT(t)[:, 0:16], TIB(t)[:, 0:16], tk(t, ["c"]), ik(t, ["c"])
         S(lambda q: q.activation(T.SV[:, 256 * t:256 * t + 256], win(t).indirect(cl), AF.Copy), r=wkey(t) + ck, w=["SV%d" % t], c=cgat(256))
-        V(lambda q: q.tensor_copy(T.RH[:], T.IDW[:].indirect(cl)), r=["IDW"] + ck, w=["RH"], c=cgat(256))
-        if SDUP:
-            S(lambda q: q.activation(T.RB[:], T.IDW[:].indirect(cl), AF.Copy), r=["IDW"] + ck, w=["RB"], c=cgat(256))
+        S(lambda q: q.activation(T.RB[:], T.IDW[:].indirect(cl), AF.Copy), r=["IDW"] + ck, w=["RB"], c=cgat(256))
         V(lambda q: q.tensor_scalar(T.CF[:], ci, -1.0, 2048.0, A.mult, A.add), r=cik, w=["CF"])
         for c in range(16):
             if c in SDUP:
                 S(lambda q, c=c: q.activation(T.EQ[:, seg[c]:seg[c + 1]], T.RB[:, 16 * c:256], AF.Square, bias=T.CF[:, c:c + 1]),
                   r=["RB", "CF"], w=["EQ%d" % c], c=cv(256 - 16 * c))
             else:
-                V(lambda q, c=c: q.tensor_scalar(T.EQ[:, seg[c]:seg[c + 1]], T.RH[:, 16 * c:256], T.CF[:, c:c + 1], 0.0, A.add, A.not_equal),
-                  r=["RH", "CF"], w=["EQ%d" % c], c=cv(256 - 16 * c, .5))
+                V(lambda q, c=c: q.tensor_scalar(T.EQ[:, seg[c]:seg[c + 1]], T.RB[:, 16 * c:256], T.CF[:, c:c + 1], 0.0, A.add, A.not_equal),
+                  r=["RB", "CF"], w=["EQ%d" % c], c=cv(256 - 16 * c))
         V(lambda q: q.tensor_tensor_scan(T.SC[:], T.EM[:], T.EQ[:], 1.0e9, A.max, A.min), r=["EM"] + ["EQ%d" % c for c in range(16)], w=["SC"], c=cv(NE, .5))
         V(lambda q: q.tensor_scalar(T.dE[:], T.SC[:].indirect(T.E16[:, 0:1]), 0.5, None, A.is_lt), r=["SC", "E16"], w=["dE"])
         V(lambda q: q.tensor_tensor(T.dF[:], T.dE[:], T.DJ[:], A.mult), r=["dE", "DJ"], w=["dF"])
@@ -605,9 +603,10 @@ def rank_program(g, core, T, topo):
     for t in range(3):
         late = tk(t, ["c"]) + ik(t, ["c"]) + [k for e in (1, 2, 3) for k in ak(t, e, ["c"]) + ek(e, ["c"])]
         if t == 0:
-            dma("g", [(T.F1[:, 0:4096], T.price[:])], r=["win0"] + late, w=["win1"], lat=10)
+            G(lambda q: q.iota(T.MK[:], [[0, 256], [256, 16]], 0, 0, allow_small_or_imprecise_dtypes=True), w=["MK"], c=cfix(8.5), after=late)
+            dma("g", [(T.F1[:, 0:4096], T.price[:])], r=["win0"], w=["win1"], lat=6, after=late)
         else:
-            dma("y", [(T["F%d" % (t + 1)][:], T["F%d" % t][:])], r=["win%d" % t] + late + (["win1d"] if t == 1 else []), w=["win%d" % (t + 1)], lat=8)
+            dma("y", [(T["F%d" % (t + 1)][:], T["F%d" % t][:])], r=["win%d" % t] + (["win1d"] if t == 1 else []), w=["win%d" % (t + 1)], lat=5, after=late)
         for e in (1, 2, 3):
             for h in HA:
                 gy(t, e, h)
@@ -622,7 +621,7 @@ def rank_program(g, core, T, topo):
             conv(48, K4)
         update(t)
         if t == 2:
-            dma("g", [(T.yp[:], T.F3[:, 0:4096])], r=["win3"], w=["yp"], lat=9)
+            dma("g", [(T.yp[:], T.F3[:, 0:4096])], r=["win3"], w=["yp"], lat=6)
         for h in HS:
             fin(t, h)
         if t < 2:

import numpy as np
from concourse.bass import DstId, RemoteDMATransfer
from concourse.mybir import dt, AluOpType, AxisListType, ActivationFunctionType

A = AluOpType
AF = ActivationFunctionType
LW = 272
CH = [(0, 16), (16, 104), (104, 192), (192, 272)]
NH = len(CH)
RT = ["svvvvvssvvvv", "vvvvvvssvvvv", "vvvvvvssvvvv"]
YR = ["sssssssvssss", "ssssvssvssss", "ssssvssssvsv"]
MR = ["vss", "sss"]
TG = [[1], [2, 3]]
NE = 2176
BIG = 32768.0
SDUP = (0, 1, 2, 3, 4, 5, 6, 7)

SCRATCH = {
    "p0": ("sbuf", [128, 4096], "bfloat16"),
    "F1": ("sbuf", [128, 4352], "float32"),
    "F2": ("sbuf", [128, 4352], "float32"),
    "F3": ("sbuf", [128, 4352], "float32"),
    "pkI": ("sbuf", [128, 768], "int32"),
    "pkJ": ("sbuf", [128, LW], "int32"),
    "PK": ("sbuf", [128, 1792], "float32"),
    "VT": ("sbuf", [128, 1024], "int32"),
    "small": ("sbuf", [128, 8], "int32"),
    "slI": ("sbuf", [128, 4], "int32"),
    "sm": ("sbuf", [128, 32], "float32"),
    "pI": ("sbuf", [128, 4], "int32"),
    "row8": ("sbuf", [128, 8], "float32"),
    "B8": ("sbuf", [128, 8], "float32"),
    "one16": ("sbuf", [128, 16], "float32"),
    "SELK": ("sbuf", [128, 2048], "bfloat16"),
    "SELH": ("sbuf", [128, 2048], "float16"),
    "ones": ("sbuf", [128, 128], "bfloat16"),
    "cB": ("sbuf", [128, 384], "bfloat16"),
    "IDN": ("sbuf", [128, 128], "float32"),
    "onesF": ("sbuf", [128, 128], "float32"),
    "IDB": ("sbuf", [128, 256], "bfloat16"),
    "BD": ("sbuf", [128, 128], "bfloat16"),
    "BE": ("sbuf", [128, 128], "bfloat16"),
    "WT": ("sbuf", [128, 128], "bfloat16"),
    "TT0": ("sbuf", [128, LW], "uint16"),
    "TT1": ("sbuf", [128, LW], "uint16"),
    "A16": ("sbuf", [128, 3 * LW], "uint16"),
    "AE": ("sbuf", [128, 3 * LW], "float32"),
    "Wt": ("sbuf", [128, LW], "int32"),
    "WF": ("sbuf", [128, LW], "float32"),
    "TI": ("sbuf", [128, LW], "int32"),
    "TJ": ("sbuf", [128, LW], "int32"),
    "Y": ("sbuf", [128, 48 * LW], "bfloat16"),
    "C": ("sbuf", [128, 16 * LW], "bfloat16"),
    "XS": ("sbuf", [128, 16 * LW], "bfloat16"),
    "XM": ("sbuf", [128, 4096], "bfloat16"),
    "SM": ("sbuf", [128, 4096], "bfloat16"),
    "MK": ("sbuf", [128, 4096], "bfloat16"),
    "SG": ("sbuf", [128, 768], "bfloat16"),
    "uI": ("sbuf", [128, 256], "int32"),
    "uJ": ("sbuf", [128, 256], "int32"),
    "qF": ("sbuf", [128, 256], "float32"),
    "qI": ("sbuf", [128, 256], "int32"),
    "KY": ("sbuf", [128, 3, 32], "float32"),
    "KB": ("sbuf", [128, 32], "float32"),
    "KM": ("sbuf", [128, 3, 32], "float32"),
    "k1": ("sbuf", [128, 32], "float32"),
    "k2": ("sbuf", [128, 32], "float32"),
    "kI": ("sbuf", [128, 32], "int32"),
    "kJ": ("sbuf", [128, 32], "int32"),
    "kF": ("sbuf", [128, 32], "float32"),
    "LU": ("sbuf", [128, 64], "uint16"),
    "i16": ("sbuf", [128, 16], "float32"),
    "L1c": ("sbuf", [128, 16], "float32"),
    "VH": ("sbuf", [128, 256], "float16"),
    "PV": ("sbuf", [128, 48], "float32"),
    "yvb": ("sbuf", [128, 384], "float32"),
    "CF": ("sbuf", [128, 16], "float32"),
    "IDW": ("sbuf", [128, 4096], "float32"),
    "RB": ("sbuf", [128, 256], "float32"),
    "IX": ("sbuf", [128, 256], "float32"),
    "QM": ("sbuf", [128, 256], "bfloat16"),
    "EQ": ("sbuf", [128, NE], "bfloat16"),
    "EM": ("sbuf", [128, NE], "bfloat16"),
    "SC": ("sbuf", [128, NE], "bfloat16"),
    "E16": ("sbuf", [128, 2], "uint16"),
    "DJ": ("sbuf", [128, 16], "float32"),
    "DJt": ("sbuf", [128, 16], "float32"),
    "dE": ("sbuf", [128, 16], "float32"),
    "dF": ("sbuf", [128, 16], "float32"),
    "dG": ("sbuf", [128, 16], "float32"),
    "SV": ("sbuf", [128, 768], "bfloat16"),
    "SL": ("sbuf", [128, 48], "uint16"),
    "LV": ("sbuf", [128, 3 * 768], "bfloat16"),
    "LL": ("sbuf", [128, 3 * 64], "uint16"),
    "sv": ("sbuf", [128, 768], "float32"),
    "g1": ("sbuf", [128, 512], "float32"),
    "t1": ("sbuf", [128, 256], "float32"),
    "i1": ("sbuf", [128, 768], "int32"),
    "Z0": ("psum", [128, 512], "float32"),
    "Z1": ("psum", [128, 512], "float32"),
    "Z2": ("psum", [128, 512], "float32"),
    "Z3": ("psum", [128, 512], "float32"),
    "ZT": ("psum", [128, 512], "float32"),
    "ZX": ("psum", [128, 512], "float32"),
    "ZB": ("psum", [128, 3, 16], "float32"),
    "ZM": ("psum", [128, 512], "float32"),
}
NDMA = 90
SEMAPHORES = ["cv", "cs", "cp", "cg", "lsem", "arr0", "arr1", "arr2"] + ["d%d" % i for i in range(NDMA)]

MODELS = [
    (0.050, 0.92e-3, 1.35e-3, 2.8e-3, 0.70e-3, 0.08, 1.0, 4.5),
    (0.045, 0.84e-3, 0.95e-3, 1.6e-3, 0.60e-3, 0.05, 0.8, 3.5),
    (0.055, 1.20e-3, 2.40e-3, 5.5e-3, 0.95e-3, 0.10, 1.3, 7.0),
    (0.050, 1.10e-3, 1.40e-3, 5.5e-3, 0.60e-3, 0.18, 0.8, 5.0),
    (0.060, 1.00e-3, 1.90e-3, 2.0e-3, 0.80e-3, 0.05, 1.0, 4.0),
    (0.065, 1.10e-3, 1.20e-3, 3.0e-3, 0.90e-3, 0.12, 1.0, 6.0),
]
TRIES = 1500


def cv(n, per=1.0):
    return (1.0, max(64, n * per), 0, 0, 0, 0)


def cgat(n):
    return (1.0, 0, n, 0, 0, 0)


def csca(n):
    return (1.0, 0, 0, n, 0, 0)


def cmm(n, k=1):
    return (0.2 * k, 0, 0, 0, k * max(64, n), 0)


def cfix(x):
    return (0, 0, 0, 0, 0, x)


def price_ops(ops, md):
    cost, lat = [], []
    for o in ops:
        c = o["cost"]
        cost.append(c[0] * md[0] + c[1] * md[1] + c[2] * md[2] + c[3] * md[3] + c[4] * md[4] + c[5])
        lat.append(o["lat"] * (md[6] if o["kind"] == "d" else 1.0) if o["kind"] != "n" else md[7])
    return cost, lat


def run_order(ops, order, cost, lat, wake):
    free, fin = {}, [0.0] * len(ops)
    end = 0.0
    for i in order:
        o = ops[i]
        e = o["e"]
        s = free.get(e, 0.0) if e != "n" else 0.0
        for p in o["full"]:
            if fin[p] + wake > s:
                s = fin[p] + wake
        f = s + cost[i]
        free[e] = f
        fin[i] = f + lat[i]
        if fin[i] > end:
            end = fin[i]
    return end


def schedule(ops, succ, prio, cost, lat, wake, window):
    m = len(ops)
    left = [len(o["full"]) + len(o["order"]) for o in ops]
    ready = [0.0] * m
    free, pend = {}, {}
    for i, o in enumerate(ops):
        free[o["e"]] = 0.0
        pend.setdefault(o["e"], [])
        if not left[i]:
            pend[o["e"]].append(i)
    names = sorted(pend)
    start = [0.0] * m
    for _ in range(m):
        t0, e = 1e30, None
        for x in names:
            if pend[x]:
                t = max(free[x], min(ready[i] for i in pend[x]))
                if t < t0:
                    t0, e = t, x
        i = max((i for i in pend[e] if ready[i] <= t0 + window), key=lambda i: (prio[i], -i))
        s = max(t0, ready[i])
        start[i] = s
        pend[e].remove(i)
        free[e] = s + cost[i] if e != "n" else 0.0
        for j, f in succ[i]:
            ready[j] = max(ready[j], s + cost[i] + (lat[i] + wake if f else 0.0))
            left[j] -= 1
            if not left[j]:
                pend[ops[j]["e"]].append(j)
    return sorted(range(m), key=lambda i: (start[i], i))


PLAN = {}


def plan(ops):
    if "order" in PLAN:
        return PLAN["order"]
    m = len(ops)
    succ = [[] for _ in ops]
    for i, o in enumerate(ops):
        for p in o["full"]:
            succ[p].append((i, True))
        for p in o["order"]:
            succ[p].append((i, False))
    priced = [price_ops(ops, md) for md in MODELS]
    cost, lat = priced[0]
    base = [0.0] * m
    for i in range(m - 1, -1, -1):
        b = 0.0
        for j, f in succ[i]:
            b = max(b, base[j] + (lat[i] + MODELS[0][5] if f else 0.0))
        base[i] = b + cost[i] + ops[i]["up"]
    rng = np.random.default_rng(2)
    ref, best, bestn = None, None, np.zeros(m)
    for k in range(TRIES):
        if k < 4:
            noise, window = np.zeros(m), (0.05, 0.15, 0.3, 0.02)[k]
        else:
            noise = bestn + rng.normal(0.0, (40.0, 8.0)[k % 2], m) * (rng.random(m) < (0.1, 0.03, 0.01)[k % 3])
            window = best[2] if k % 5 else float(rng.choice([0.02, 0.05, 0.1, 0.2]))
        order = schedule(ops, succ, [base[i] + float(noise[i]) for i in range(m)], cost, lat, MODELS[0][5], window)
        ts = [run_order(ops, order, c, l, md[5]) for (c, l), md in zip(priced, MODELS)]
        if ref is None:
            ref = ts
        sc = sum(a / b for a, b in zip(ts, ref))
        if best is None or sc < best[0]:
            best, bestn = (sc, order, window, ts), noise
    PLAN["order"] = best[1]
    PLAN["ts"] = (ref, best[3])
    return best[1]


def rank_program(g, core, T, topo):
    rank = T.rank_of(core)
    if rank is None:
        return
    n = len(T.cores)
    Q = {"v": g.vector, "s": g.scalar, "p": g.tensor, "g": g, "y": g.sync}
    CSEM = {"v": "cv", "s": "cs", "p": "cp", "g": "cg"}
    ops = []
    lastw, readers = {}, {}

    def add(e, kind, body, r, w, cost, lat=0.0, up=0.0, after=()):
        i = len(ops)
        full, order = set(), set()
        comp = kind == "c"
        for k in list(r) + list(after):
            if k in lastw:
                full.add(lastw[k])
        for k in w:
            if k in lastw:
                full.add(lastw[k])
            for x in readers.get(k, []):
                if comp and ops[x]["e"] == e and ops[x]["kind"] == "c":
                    order.add(x)
                else:
                    full.add(x)
        full.discard(i)
        ops.append({"e": e, "kind": kind, "body": body, "full": sorted(full), "order": sorted(order - full),
                    "cost": cost, "lat": lat, "up": up})
        for k in r:
            readers.setdefault(k, []).append(i)
        for k in w:
            lastw[k] = i
            readers[k] = []

    def V(f, r=(), w=(), c=cv(1)):
        add("v", "c", [f], r, w, c)

    def S(f, r=(), w=(), c=cv(1)):
        add("s", "c", [f], r, w, c)

    def PE(fs, r=(), w=(), c=None):
        fs = fs if isinstance(fs, list) else [fs]
        add("p", "c", fs, r, w, c if c else cmm(16, len(fs)))

    def G(f, r=(), w=(), c=cfix(0.2), after=()):
        add("g", "c", [f], r, w, c, after=after)

    def dma(e, pairs, r=(), w=(), lat=2.3, up=0.0, after=()):
        add(e, "d", pairs, r, w, cfix(0.06 * len(pairs)), lat, up, after)

    RF, GF, RQ, INC, WTF, SLF, SB, HF, C14, C15 = 0, 1, 2, 3, 4, 8, 12, 16, 17, 18
    sm = T.sm
    col = lambda c: sm[:, c:c + 1]
    HA = range(NH)
    HS = range(1, NH)
    ALL = ["c"] + list(HS)
    part = lambda h: ["c"] if h == 0 else [h]
    TT = lambda t: T["TT%d" % (t % 2)]
    tk = lambda t, hs: ["TT%d_%s" % (t % 2, h) for h in hs]
    TIB = lambda t: T.TI if t % 2 == 0 else T.TJ
    ik = lambda t, hs: [("TI_%s" if t % 2 == 0 else "TJ_%s") % h for h in hs]
    ek = lambda e, hs: ["AE%d_%s" % (e, h) for h in hs]
    win = lambda t: T.p0[:, 0:4096] if t == 0 else T["F%d" % t][:, 0:4096]
    wkey = lambda t: ["win%d" % t]

    def alist(t, e, a, b):
        return TT(t - 1)[:, a:b] if e == 1 and t > 0 else T.A16[:, LW * (e - 1) + a:LW * (e - 1) + b]

    def ak(t, e, hs):
        return tk(t - 1, hs) if e == 1 and t > 0 else ["A16_%d_%s" % (e, h) for h in hs]

    dma("y", [(T.pkJ[:, 16:LW], T.packs[:, 768:1024]), (T.pkJ[:, 0:16], T.packs[0:128:16, 768:1024])], w=["pkJ"], lat=3, up=2000)
    dma("y", [(T.slI[:, 0:3], T.slack[:])], w=["slI"], lat=3, up=1800)
    dma("y", [(T.p0[:], T.price[:])], w=["win0"], lat=5, up=1600)
    dma("y", [(T.TI[:, 16:LW], T.lots[:]), (T.TI[:, 0:16], T.lots[0:128:16, :])], w=ik(0, ALL), lat=4, up=1500)
    dma("s", [(T.VT[r:128:16, :], T.prev[:]) for r in range(8)], w=["VTa"], lat=7)
    dma("y", [(T.VT[r:128:16, :], T.prev[:]) for r in range(8, 16)], w=["VTb"], lat=7)
    dma("y", [(T.pkI[:], T.packs[:, 0:768])], w=["pkI"], lat=9)
    dma("y", [(T.small[:, 0:1], T.inc[:]), (T.small[:, 4:5], T.wt[:])], w=["smallI"], lat=9)
    VTR = ["VTa", "VTb"]

    G(lambda q: q.iota(T.pI[:, 0:1], [[1, 1]], 0, 1), w=["pI"])
    G(lambda q: q.iota(T.row8[:], [[1, 8]], 0, 0, allow_small_or_imprecise_dtypes=True), w=["row8"])
    G(lambda q: q.iota(T.i16[:], [[16, 16]], 0, 0, allow_small_or_imprecise_dtypes=True), w=["i16"])

    V(lambda q: q.memset(T.SELK[:], 0.0), w=["SELK"], c=cv(1024))
    V(lambda q: q.memset(T.one16[:], 1.0), w=["one16"])
    V(lambda q: q.memset(T.ones[:], 1.0), w=["ones"])
    for i, x in enumerate((-8.5, -1.0, 15.0)):
        V(lambda q, i=i, x=x: q.memset(T.cB[:, 128 * i:128 * i + 128], x * BIG), w=["cB%d" % i])
    V(lambda q: q.tensor_scalar(T.pI[:, 1:2], T.pI[:, 0:1], 15, None, A.bitwise_and), r=["pI"], w=["pI1"])
    V(lambda q: q.tensor_scalar(T.pI[:, 2:3], T.pI[:, 0:1], 4, None, A.logical_shift_right), r=["pI"], w=["pI2"])
    V(lambda q: q.tensor_copy(col(RF), T.pI[:, 1:2]), r=["pI1"], w=["RF"])
    V(lambda q: q.tensor_copy(col(GF), T.pI[:, 2:3]), r=["pI2"], w=["GF"])
    V(lambda q: q.tensor_scalar(T.B8[:], T.row8[:], col(GF), None, A.is_equal), r=["row8", "GF"], w=["B8"])
    V(lambda q: q.tensor_scalar(T.L1c[:], T.i16[:], col(RF), None, A.add), r=["i16", "RF"], w=["L1c"])
    for gg in range(8):
        V(lambda q, gg=gg: q.tensor_scalar(T.SELK[:, 16 * gg:16 * gg + 129 * 15 + 1:129], T.one16[:],
                                           T.B8[:, gg:gg + 1], BIG, A.mult, A.mult),
          r=["one16", "B8", "SELK"], w=["SELK%d" % gg])
    SELK = ["SELK"] + ["SELK%d" % gg for gg in range(8)]
    V(lambda q: q.tensor_copy(T.A16[:, 0:LW], T.pkJ[:]), r=["pkJ"], w=ak(0, 1, ALL), c=cv(LW))
    V(lambda q: q.tensor_copy(sm[:, SLF:SLF + 3], T.slI[:, 0:3]), r=["slI"], w=["SLF"])
    V(lambda q: q.tensor_copy(T.TT0[:], T.TI[:]), r=ik(0, ALL), w=tk(0, ALL), c=cv(LW))
    V(lambda q: q.tensor_scalar(T.AE[:, 0:LW], T.pkJ[:], 4096.0, None, A.add), r=["pkJ"], w=ek(1, ALL), c=cv(LW))
    V(lambda q: q.tensor_copy(T.VH[:], T.VT[:, 768:1024]), r=VTR, w=["VH"], c=cv(256))
    V(lambda q: q.tensor_scalar(T.SELH[:], T.SELK[:], 1.0 / BIG, None, A.mult), r=SELK, w=["SELH"], c=cv(1024))
    for e in range(3):
        V(lambda q, e=e: q.memset(col(SB + e), 0.5 - 4096.0 * (e + 1)), w=["SB%d" % e])
    V(lambda q: q.memset(col(HF), -0.5), w=["HF"])
    V(lambda q: q.memset(T.onesF[:], 1.0), w=["onesF"], c=cv(128))
    G(lambda q: q.affine_select(T.IDB[:, 0:128], T.ones[:], [[-1, 128]], A.is_equal, 0.0, 0, 1), r=["ones"], w=["IDB"], c=cfix(0.45))
    V(lambda q: q.tensor_scalar(T.IDB[:, 128:256], T.IDB[:, 0:128], -1.0, None, A.mult), r=["IDB"], w=["IDM"])
    G(lambda q: q.iota(T.IDW[:], [[1, 4096]], -2048, 0, allow_small_or_imprecise_dtypes=True), w=["IDW"], c=cfix(8.5))
    G(lambda q: q.iota(T.IX[:], [[1, 256]], 0, 0, allow_small_or_imprecise_dtypes=True), w=["IX"], c=cfix(0.7))
    G(lambda q: q.affine_select(T.IDN[:], T.onesF[:], [[-1, 128]], A.is_equal, 0.0, 0, 1), r=["onesF"], w=["IDN"], c=cfix(0.45))
    V(lambda q: q.tensor_copy(T.PK[:, 768:1024], T.pkJ[:, 16:LW]), r=["pkJ"], w=["PKb"], c=cv(256))
    V(lambda q: q.tensor_copy(T.PK[:, 0:768], T.pkI[:]), r=["pkI"], w=["PKa"], c=cv(768))
    V(lambda q: q.memset(T.F1[:, 4096:4352], 0.0), w=["win1d"], c=cv(256))
    V(lambda q: q.tensor_scalar(col(RQ), col(RF), 1.0, None, A.add), r=["RF"], w=["RQ"])
    V(lambda q: q.tensor_scalar(T.QM[:], T.IX[:], col(RQ), 1.0e9, A.is_equal, A.mult), r=["IX", "RQ"], w=["QM"], c=cv(256))
    seg = [256 * c - 8 * c * (c - 1) for c in range(17)]
    dma("y", [(T.EM[:, seg[c]:seg[c + 1]], T.QM[:, 0:256 - 16 * c]) for c in range(16)], r=["QM"], w=["EM"])
    V(lambda q: q.tensor_scalar(col(C14), col(RF), -8.0, 248.0, A.mult, A.add), r=["RF"], w=["c14"])
    V(lambda q: q.tensor_tensor(col(C15), col(C14), col(RF), A.mult), r=["c14", "RF"], w=["c15"])
    V(lambda q: q.tensor_scalar(T.E16[:, 0:1], col(C15), 255.0, None, A.add), r=["c15"], w=["E16"])
    V(lambda q: q.tensor_scalar(T.DJt[:], T.L1c[:], 4096.0, None, A.add), r=["L1c"], w=["DJt"])
    V(lambda q: q.tensor_scalar(T.dF[:], T.DJt[:], 4350.5, None, A.is_lt), r=["DJt"], w=["dF"])
    V(lambda q: q.tensor_tensor(T.DJ[:], T.dF[:], T.DJt[:], A.mult), r=["dF", "DJt"], w=["DJ"])
    V(lambda q: q.tensor_scalar(col(INC), T.small[:, 0:1], 1.0 / 64, None, A.mult), r=["smallI"], w=["INC"])
    V(lambda q: q.tensor_copy(col(WTF), T.small[:, 4:5]), r=["smallI"], w=["WTF"])
    G(lambda q: q.affine_select(T.BD[:], T.ones[:], [[-16, 8], [0, 16]], A.is_ge, 0.0, 0, 1), r=["ones"], w=["BD"], c=cfix(0.45))
    G(lambda q: q.affine_select(T.BE[:], T.BD[:], [[16, 8], [0, 16]], A.is_ge, 0.0, 15, -1), r=["BD"], w=["BE"], c=cfix(0.45))
    V(lambda q: q.tensor_scalar(T.WT[:], T.BE[:], col(WTF), None, A.mult), r=["BE", "WTF"], w=["WT"])

    KY, KB = T.KY, T.KB
    K2 = [(KY[:, 0, 16:32], "KY01", 4096.0), (KY[:, 1, 0:16], "KY10", 8192.0)]
    K3 = [(KY[:, 1, 16:32], "KY11", 8192.0), (KY[:, 2, 0:16], "KY20", 12288.0), (KB[:, 0:16], "KB0", 0.0)]
    K4 = [(KY[:, 2, 16:32], "KY21", 12288.0), (KB[:, 16:32], "KB1", 0.0)]

    def conv(dst, keys):
        PE([lambda q, k=k: q.matmul(T.ZM[:, 256:272], T.SELH[:, 128 * k:128 * k + 128], T.VH[:, k:256:16], k == 0, k == 15)
            for k in range(16)], r=["VH", "SELH"], w=["bM"])
        if dst < 48:
            V(lambda q: q.tensor_scalar(T.LU[:, dst:dst + 16], T.ZM[:, 256:272], 1.0 / 16, None, A.mult), r=["bM"], w=["LU%d" % dst])
        V(lambda q: q.tensor_scalar(T.kF[:, 0:16], T.ZM[:, 256:272], 1.0 / 16, None, A.mult), r=["bM"], w=["kF"])
        for ap, nm, off in keys:
            S(lambda q, ap=ap, off=off: q.activation(ap, T.kF[:, 0:16], AF.Copy, bias=off), r=["kF"], w=[nm])

    def parents(src):
        V(lambda q: q.tensor_copy(T.VH[:], T.VT[:, 0:1024].indirect(T.LU[:, src:src + 16])), r=VTR + ["LU%d" % src], w=["VH"], c=cgat(256))

    def newest(t):
        base = 768.0 + 256 * t
        S(lambda q: q.activation(KY[:, 0, 0:16], T.L1c[:], AF.Copy, bias=base + 4096.0), r=["L1c"], w=["KY00"])

    def package(t, e):
        c, b = LW * (e - 1) + 16, 16 * (e - 1)
        S(lambda q: q.activation(T.AE[:, c:c + 256], T.PK[:, 0:1024 + 256 * t].indirect(T.LU[:, b:b + 16]), AF.Copy, bias=4096.0 * e),
          r=["PKa", "PKb"] + ["PK%d_%d" % (i, h) for i in range(t) for h in HS] + ["LU%d" % b], w=ek(e, HS), c=cgat(256))
        V(lambda q: q.tensor_scalar(T.A16[:, c:c + 256], T.AE[:, c:c + 256], -4096.0 * e, None, A.add),
          r=ek(e, HS), w=ak(t, e, HS), c=cv(256))

    def clist(t, e):
        if e == 0:
            dma("y", [(TT(t)[:, 0:16], TT(t)[t:128:16, 16:LW])], r=tk(t, HS), w=tk(t, ["c"]))
            dma("y", [(TIB(t)[:, 0:16], TIB(t)[t:128:16, 16:LW])], r=ik(t, HS), w=ik(t, ["c"]))
        else:
            o = LW * (e - 1)
            dma("y", [(alist(t, e, 0, 16), alist(t, e, 16, LW)[t:128:16, :])], r=ak(t, e, HS), w=ak(t, e, ["c"]))
            dma("y", [(T.AE[:, o:o + 16], T.AE[t:128:16, o + 16:o + LW])], r=ek(e, HS), w=ek(e, ["c"]))

    blocks = lambda m: [(x, min(x + 512, 16 * m)) for x in range(0, 16 * m, 512)]

    def gy(t, e, h):
        a, b = CH[h]
        o = 16 * (LW * (e - 1) + a)
        out, lst = T.Y[:, o:o + 16 * (b - a)], win(t).indirect(alist(t, e, a, b))
        r, w, c = wkey(t) + ak(t, e, part(h)) + ["SLF"], ["Y%d_%d" % (e, h)], cgat(16 * (b - a))
        if YR[t][NH * (e - 1) + h] == "v":
            V(lambda q: q.tensor_scalar(out, lst, col(SLF + t), None, A.add), r=r, w=w, c=c)
        else:
            S(lambda q: q.activation(out, lst, AF.Identity, bias=col(SLF + t)), r=r, w=w, c=c)

    def gx(t, e, h):
        a, b = CH[h]
        o = 16 * LW * (e - 1)
        c0, c1 = 16 * a, 16 * b
        m = b - a
        z = T["Z%d" % h]
        lst = win(t).indirect(TT(t)[:, a:b])
        r = wkey(t) + tk(t, part(h))
        ck = ["C%d_%d" % (h, x) for x, y in blocks(m)]
        if RT[t][NH * (e - 1) + h] == "v":
            V(lambda q: q.tensor_tensor(T.C[:, c0:c1], lst, T.Y[:, o + c0:o + c1], A.is_gt), r=r + ["Y%d_%d" % (e, h)], w=ck, c=cgat(16 * m))
            sh = 0
        else:
            S(lambda q: q.activation(T.XS[:, c0:c1], lst, AF.Copy), r=r, w=["XS%d" % h], c=cgat(16 * m))
            for x, y in blocks(m):
                PE([lambda q, x=x, y=y: q.matmul(T.ZX[:, 0:y - x], T.IDB[:, 0:128], T.XS[:, c0 + x:c0 + y], True, False),
                    lambda q, x=x, y=y: q.matmul(T.ZX[:, 0:y - x], T.IDB[:, 128:256], T.Y[:, o + c0 + x:o + c0 + y], False, True)],
                   r=["XS%d" % h, "IDB", "IDM", "Y%d_%d" % (e, h)], w=["bX"], c=cmm(y - x, 2))
                S(lambda q, x=x, y=y: q.activation(T.C[:, c0 + x:c0 + y], T.ZX[:, 0:y - x], AF.Sign, bias=col(HF)),
                  r=["bX", "HF"], w=["C%d_%d" % (h, x)], c=cv(y - x))
            sh = 1
        PE([lambda q: q.matmul(z[:, 0:m], T.cB[0:1, 128 * sh:128 * sh + 128], T.ones[0:1, 0:m], True, False)] +
           [lambda q, k=k: q.matmul(z[:, 0:m], T.SELK[:, 128 * k:128 * k + 128], T.C[:, c0 + k:c1:16], False, k == 15)
            for k in range(16)], r=ck + ["cB%d" % sh, "ones"] + SELK, w=["bZ%d" % h], c=cmm(m, 17))

    def tops(t, e, h):
        a, b = CH[h]
        m = b - a
        z, ti = T["Z%d" % h], TIB(t)
        o = LW * (e - 1)
        V(lambda q: q.tensor_tensor(T.ZT[:, a:b], z[:, 0:m], T.AE[:, o + a:o + b], A.min), r=["bZ%d" % h] + ek(e, part(h)), w=["bT%d" % h], c=cv(m))
        cur, ck = (ti, ik(t, part(h))) if e == 1 else (T.Wt, ["W%d" % h])
        if e < 3 or h == 0:
            V(lambda q: q.tensor_tensor(T.Wt[:, a:b], T.ZT[:, a:b], cur[:, a:b], A.max), r=["bT%d" % h] + ck, w=["W%d" % h], c=cv(m))
        else:
            V(lambda q: q.tensor_tensor(T.WF[:, a:b], T.ZT[:, a:b], cur[:, a:b], A.max), r=["bT%d" % h] + ck, w=["WF%d" % h], c=cv(m))
            V(lambda q: q.tensor_copy(T.Wt[:, a:b], T.WF[:, a:b]), r=["WF%d" % h], w=["W%d" % h], c=cv(m))
        V(lambda q: q.tensor_scalar(ti[:, a:b], T.Wt[:, a:b], 4095, None, A.bitwise_and), r=["W%d" % h], w=ik(t, part(h)), c=cv(m))
        V(lambda q: q.tensor_copy(TT(t)[:, a:b], ti[:, a:b]), r=ik(t, part(h)), w=tk(t, part(h)), c=cv(m))

    def fin(t, h):
        a, b = CH[h]
        p = 1024 + 256 * t - 16
        V(lambda q: q.tensor_copy(T.PK[:, p + a:p + b], TIB(t)[:, a:b]), r=ik(t, [h]), w=["PK%d_%d" % (t, h)], c=cv(b - a))
        if t < 2:
            S(lambda q: q.activation(T.AE[:, a:b], T.PK[:, p + a:p + b], AF.Copy, bias=4096.0), r=["PK%d_%d" % (t, h)], w=ek(1, [h]), c=cv(b - a))
        for e in range(3):
            S(lambda q, e=e: q.activation(T.SG[:, 256 * e + a - 16:256 * e + b - 16], T.WF[:, a:b], AF.Sign, bias=col(SB + e)),
              r=["WF%d" % h, "SB%d" % e], w=["SG%d_%d" % (e, h)], c=cv(b - a))

    def gm(t, h):
        a, b = CH[h]
        x, y = 16 * (a - 16), 16 * (b - 16)
        lst = win(t).indirect(TT(t)[:, a:b])
        r, w, c = wkey(t) + tk(t, [h]), ["XM%d" % h], cgat(y - x)
        if MR[t][h - 1] == "v":
            V(lambda q: q.tensor_copy(T.XM[:, x:y], lst), r=r, w=w, c=c)
        else:
            S(lambda q: q.activation(T.XM[:, x:y], lst, AF.Copy), r=r, w=w, c=c)
        V(lambda q: q.tensor_tensor_scan(T.SM[:, x:y], T.MK[:, x:y], T.XM[:, x:y], 0.0, A.min, A.max),
          r=["MK", "XM%d" % h], w=["SM%d" % h], c=cv((y - x) // 2))

    def tnew(t, hs):
        a, b = CH[hs[0]][0], CH[hs[-1]][1]
        x, y = a - 16, b - 16
        m = b - a
        nm = str(hs[0])
        uk = ["bT%d" % h for h in hs]
        PE(lambda q: q.matmul(T.ZM[:, x:y], T.WT[:], T.SM[:, 16 * x + 15:16 * y:16], True, True), r=["WT"] + ["SM%d" % h for h in hs], w=["bM"], c=cmm(m))
        V(lambda q: q.tensor_copy(T.uI[:, x:y], T.ZM[:, x:y]), r=["bM"], w=["uI" + nm], c=cv(m))
        V(lambda q: q.tensor_scalar(T.uJ[:, x:y], T.uI[:, x:y], 1023, None, A.bitwise_and), r=["uI" + nm], w=["uJ" + nm], c=cv(m))
        V(lambda q: q.tensor_scalar(T.ZT[:, a:b], T.uJ[:, x:y], 2.0, 33.0, A.mult, A.add), r=["uJ" + nm], w=uk, c=cv(m))
        V(lambda q: q.tensor_tensor(T.qF[:, x:y], T.ZT[:, a:b], TIB(t)[:, a:b], A.mult), r=uk + ik(t, hs), w=["qF" + nm], c=cv(m))
        V(lambda q: q.tensor_scalar(T.qI[:, x:y], T.qF[:, x:y], 2464.0 * (t + 1), None, A.add), r=["qF" + nm], w=["qI" + nm], c=cv(m))
        V(lambda q: q.tensor_scalar(TIB(t + 1)[:, a:b], T.qI[:, x:y], 5, 4095, A.logical_shift_right, A.bitwise_and),
          r=["qI" + nm], w=ik(t + 1, hs), c=cv(m))
        V(lambda q: q.tensor_copy(TT(t + 1)[:, a:b], TIB(t + 1)[:, a:b]), r=ik(t + 1, hs), w=tk(t + 1, hs), c=cv(m))

    def bind(t):
        PE([lambda q: q.matmul(T.ZB[:], T.cB[0:1, 256:384], T.ones[0:1, 0:48], True, False)] +
           [lambda q, k=k: q.matmul(T.ZB[:], T.SELK[:, 128 * k:128 * k + 128], T.SG[:, k:768:16], False, k == 15) for k in range(16)],
           r=["SG%d_%d" % (e, h) for e in range(3) for h in HS] + SELK + ["cB2", "ones"], w=["bB"])
        c = 16 if t == 2 else 32
        ds = range(c // 16)
        for d in ds:
            V(lambda q, d=d: q.tensor_tensor(T.KM[:, :, 16 * d:16 * d + 16], T.ZB[:], KY[:, :, 16 * d:16 * d + 16], A.min),
              r=["bB"] + ["KY%d%d" % (e, d) for e in range(3)], w=["KM%d" % d])
        V(lambda q: q.tensor_tensor(T.k1[:, 0:c], T.KM[:, 0, 0:c], T.KM[:, 1, 0:c], A.max), r=["KM%d" % d for d in ds], w=["k1"])
        V(lambda q: q.tensor_tensor(T.k2[:, 0:c], T.k1[:, 0:c], T.KM[:, 2, 0:c], A.max), r=["k1"] + ["KM%d" % d for d in ds], w=["k2"])
        V(lambda q: q.tensor_tensor(T.kI[:, 0:c], T.k2[:, 0:c], KB[:, 0:c], A.max), r=["k2"] + ["KB%d" % d for d in ds], w=["kI"])
        V(lambda q: q.tensor_scalar(T.kJ[:, 0:c], T.kI[:, 0:c], 4095, None, A.bitwise_and), r=["kI"], w=["kJ"])
        if t < 2:
            V(lambda q: q.tensor_copy(T.LU[:, 16:48], T.kJ[:]), r=["kJ"], w=["LU16", "LU32"])
            V(lambda q: q.tensor_copy(T.kF[:], T.kJ[:]), r=["kJ"], w=["kF"])
            S(lambda q: q.activation(T.PV[:, 16 * t:16 * t + 16], T.kF[:, 0:16], AF.Copy), r=["kF"], w=["PV%d" % t])
            S(lambda q: q.activation(KY[:, 0, 16:32], T.kF[:, 0:16], AF.Copy, bias=4096.0), r=["kF"], w=["KY01"])
            S(lambda q: q.activation(KY[:, 1, :], T.kF[:], AF.Copy, bias=8192.0), r=["kF"], w=["KY10", "KY11"])
            S(lambda q: q.activation(KY[:, 2, 0:16], T.kF[:, 16:32], AF.Copy, bias=12288.0), r=["kF"], w=["KY20"])
            S(lambda q: q.activation(KB[:, 0:16], T.kF[:, 16:32], AF.Copy), r=["kF"], w=["KB0"])
            newest(t + 1)
        else:
            V(lambda q: q.tensor_copy(T.PV[:, 32:48], T.kJ[:, 0:16]), r=["kJ"], w=["PV2"])

    def outv(t):
        PE(lambda q: q.matmul(T.ZM[0:16, 384:512], T.PV[:, 16 * t:16 * t + 16], T.IDN[:], True, True), r=["PV%d" % t, "IDN"], w=["bM"], c=cmm(128, 4))
        V(lambda q: q.tensor_copy(T.yvb[0:16, 128 * t:128 * t + 128], T.ZM[0:16, 384:512]), r=["bM"], w=["yvb%d" % t], c=cv(128))
        for i, e in enumerate(("y", "s") if t == 2 else ("y",)):
            gs = range(8)[i::2] if t == 2 else range(8)
            dma(e, [(T.yv[gg:gg + 1, 256 * t:256 * t + 256], T.yvb[0:16, 128 * t + 16 * gg:128 * t + 16 * gg + 16]) for gg in gs],
                r=["yvb%d" % t], w=["yv%d_%d" % (t, i)])

    def outh(t, hs):
        a, b = CH[hs[0]][0] - 16, CH[hs[-1]][1] - 16
        p = 1024 + 256 * t
        dma("y", [(T.yh[:, 256 * t + a:256 * t + b], T.PK[:, p + a:p + b])], r=["PK%d_%d" % (t, h) for h in hs], w=["yh%d_%d" % (t, a)])

    def dedupe(t):
        cl, ci, ck, cik = TT(t)[:, 0:16], TIB(t)[:, 0:16], tk(t, ["c"]), ik(t, ["c"])
        S(lambda q: q.activation(T.SV[:, 256 * t:256 * t + 256], win(t).indirect(cl), AF.Copy), r=wkey(t) + ck, w=["SV%d" % t], c=cgat(256))
        S(lambda q: q.activation(T.RB[:], T.IDW[:].indirect(cl), AF.Copy), r=["IDW"] + ck, w=["RB"], c=cgat(256))
        V(lambda q: q.tensor_scalar(T.CF[:], ci, -1.0, 2048.0, A.mult, A.add), r=cik, w=["CF"])
        for c in range(16):
            if c in SDUP:
                S(lambda q, c=c: q.activation(T.EQ[:, seg[c]:seg[c + 1]], T.RB[:, 16 * c:256], AF.Square, bias=T.CF[:, c:c + 1]),
                  r=["RB", "CF"], w=["EQ%d" % c], c=cv(256 - 16 * c))
            else:
                V(lambda q, c=c: q.tensor_scalar(T.EQ[:, seg[c]:seg[c + 1]], T.RB[:, 16 * c:256], T.CF[:, c:c + 1], 0.0, A.add, A.not_equal),
                  r=["RB", "CF"], w=["EQ%d" % c], c=cv(256 - 16 * c))
        V(lambda q: q.tensor_tensor_scan(T.SC[:], T.EM[:], T.EQ[:], 1.0e9, A.max, A.min), r=["EM"] + ["EQ%d" % c for c in range(16)], w=["SC"], c=cv(NE, .5))
        V(lambda q: q.tensor_scalar(T.dE[:], T.SC[:].indirect(T.E16[:, 0:1]), 0.5, None, A.is_lt), r=["SC", "E16"], w=["dE"])
        V(lambda q: q.tensor_tensor(T.dF[:], T.dE[:], T.DJ[:], A.mult), r=["dE", "DJ"], w=["dF"])
        V(lambda q: q.tensor_tensor(T.dG[:], T.dF[:], ci, A.max), r=["dF"] + cik, w=["dG"])
        V(lambda q: q.tensor_copy(T.SL[:, 16 * t:16 * t + 16], T.dG[:]), r=["dG"], w=["SL%d" % t])

    others = [d for d in range(n) if d != rank]
    common = [e for e in topo.engines(core, T.cores[others[0]]) if all(e in topo.engines(core, T.cores[d]) for d in others)]
    mask = sum(1 << e for e in common)

    def send(t):
        for key, buf, land, w, st in (("SV%d" % t, T.SV, T.LV, 256, 768), ("SL%d" % t, T.SL, T.LL, 16, 64)):
            ids, dsts = [], []
            for d in others:
                rid, pid = topo.addr(T.cores[d])[0:2]
                slot = (rank - d - 1) % n
                ids.append(DstId(rid=rid, pnc=pid))
                dsts.append(land[:, st * t + w * slot:st * t + w * slot + w])
            tr = RemoteDMATransfer(dst_ids=ids, dma_engine_mask=mask, remote_sem=T.sem["arr%d" % t],
                                   srcs=[buf[:, w * t:w * t + w]], dsts=dsts, alu_op=0)
            add("g", "r", tr, [key], ["sent" + key], cfix(1.0))
        add("n", "n", ("arr%d" % t, 2 * len(common) * len(others)), ["sentSV%d" % t, "sentSL%d" % t], ["LV%d" % t], cfix(0.0), 1.0)

    def update(t):
        F = T["F%d" % (t + 1)]
        fk = "win%d" % (t + 1)
        L = lambda a, b: T.LL[:, 64 * t + 16 * a:64 * t + 16 * b]
        lk = "LV%d" % t
        cols = lambda i: slice(256 * i, 256 * i + 256)
        S(lambda q: q.activation(T.sv[:], T.LV[:, 768 * t:768 * t + 768], AF.Copy, scale=col(INC)), r=[lk, "INC"], w=["sv"], c=cv(768))
        fr = [fk, "win1d", lk] if t == 0 else [fk, lk]
        for i in range(2):
            S(lambda q, i=i: q.activation(T.g1[:, cols(i)], F[:].indirect(L(i, i + 1)), AF.Copy), r=fr, w=["g1_%d" % i], c=cgat(256))
            V(lambda q, i=i: q.tensor_tensor(F[:].indirect(L(i, i + 1)), T.g1[:, cols(i)], T.sv[:, cols(i)], A.add), r=["g1_%d" % i, "sv", lk], w=[fk], c=csca(256))
        V(lambda q: q.tensor_tensor(T.t1[:], F[:].indirect(L(2, 3)), T.sv[:, 512:768], A.add), r=fr + ["sv"], w=["t1"], c=cgat(256))
        V(lambda q: q.tensor_scalar(T.i1[:, 512:768], T.t1[:], -0.4921875, 255.0, A.add, A.min), r=["t1"], w=["i1b"], c=cv(256))
        V(lambda q: q.tensor_copy(F[:].indirect(L(2, 3)), T.i1[:, 512:768]), r=["i1b", lk], w=[fk], c=csca(256))
        V(lambda q: q.tensor_scalar(T.i1[:, 0:512], F[:].indirect(L(0, 2)), -0.4921875, 255.0, A.add, A.min), r=[fk, lk], w=["i1a"], c=cgat(512))
        for i in range(2):
            V(lambda q, i=i: q.tensor_copy(F[:].indirect(L(i, i + 1)), T.i1[:, cols(i)]), r=["i1a", lk], w=[fk], c=csca(256))

    newest(0)
    conv(16, K2)
    parents(16)
    conv(32, K3)
    package(0, 2)
    package(0, 3)
    clist(0, 2)
    clist(0, 3)
    for t in range(3):
        late = tk(t, ["c"]) + ik(t, ["c"]) + [k for e in (1, 2, 3) for k in ak(t, e, ["c"]) + ek(e, ["c"])]
        if t == 0:
            G(lambda q: q.iota(T.MK[:], [[0, 256], [256, 16]], 0, 0, allow_small_or_imprecise_dtypes=True), w=["MK"], c=cfix(8.5), after=late)
            dma("g", [(T.F1[:, 0:4096], T.price[:])], r=["win0"], w=["win1"], lat=6, after=late)
        else:
            dma("y", [(T["F%d" % (t + 1)][:], T["F%d" % t][:])], r=["win%d" % t] + (["win1d"] if t == 1 else []), w=["win%d" % (t + 1)], lat=5, after=late)
        for e in (1, 2, 3):
            for h in HA:
                gy(t, e, h)
            for h in HA:
                gx(t, e, h)
            for h in HA:
                tops(t, e, h)
        dedupe(t)
        send(t)
        if t < 2:
            parents(32)
            conv(48, K4)
        update(t)
        if t == 2:
            dma("g", [(T.yp[:], T.F3[:, 0:4096])], r=["win3"], w=["yp"], lat=6)
        for h in HS:
            fin(t, h)
        if t < 2:
            for h in HS:
                gm(t, h)
            for hs in TG:
                tnew(t, hs)
            clist(t + 1, 1)
            clist(t + 1, 0)
            outh(t, list(HS))
        else:
            for h in HS:
                outh(t, [h])
        bind(t)
        outv(t)
        if t < 2:
            package(t + 1, 2)
            package(t + 1, 3)
            clist(t + 1, 2)
            clist(t + 1, 3)

    order = plan(ops)
    total, snap, tok = {}, {}, {}
    seen = {e: {} for e in Q}
    nd = [0]

    def merge(d, s, v):
        if d.get(s, 0) < v:
            d[s] = v

    def sync(e, toks):
        best = {}
        for s, v in toks:
            if seen[e].get(s, 0) < v:
                merge(best, s, v)
        for s in sorted(best):
            if any(o != s and best[o] and snap.get((o, best[o]), {}).get(s, 0) >= best[s] for o in best):
                best[s] = 0
        for s in sorted(best):
            v = best[s]
            if v:
                Q[e].wait_ge(T.sem[s], v)
                merge(seen[e], s, v)
                for o, w in snap.get((s, v), {}).items():
                    merge(seen[e], o, w)

    for i in order:
        o = ops[i]
        e, kind, body = o["e"], o["kind"], o["body"]
        if kind == "n":
            total[body[0]] = body[1]
            tok[i] = body
            continue
        sync(e, [tok[p] for p in o["full"] if p in tok])
        if kind == "c":
            s = CSEM[e]
            for f in body:
                f(Q[e]).then_inc(T.sem[s], 1)
                total[s] = total.get(s, 0) + 1
                snap[(s, total[s])] = dict(seen[e])
            tok[i] = (s, total[s])
        elif kind == "d":
            s = "d%d" % nd[0]
            nd[0] += 1
            for out, in_ in body:
                Q[e].dma_start(out, in_).then_inc(T.sem[s], 16)
            total[s] = 16 * len(body)
            tok[i] = (s, total[s])
            snap[tok[i]] = dict(seen[e])
        else:
            g.remote_dma_fused([body], local_sem=T.sem.lsem)
            total["lsem"] = total.get("lsem", 0) + len(common)
    for s in sorted(total):
        if seen["g"].get(s, 0) < total[s]:
            g.wait_ge(T.sem[s], total[s])
